import numpy as np
import ml_dtypes


def mxq(x, axis, fmt="e4m3"):
    dtype, down = {"e4m3": (ml_dtypes.float8_e4m3fn, 7), "e5m2": (ml_dtypes.float8_e5m2, 14)}[fmt]
    v = np.moveaxis(np.asarray(x, np.float32).astype(ml_dtypes.bfloat16).astype(np.float64), axis, -1)
    blocks = v.reshape(v.shape[:-1] + (-1, 32))
    amax = np.abs(blocks).max(-1, keepdims=True)
    byte = np.maximum(np.where(amax > 0, np.frexp(amax)[1] - 1 + 127, 0) - down, 1)
    scale = np.exp2(byte - 127.0)
    codes = (blocks / scale).astype(np.float32).astype(dtype).astype(np.float64)
    return np.moveaxis((codes * scale).reshape(v.shape), -1, axis)


WIDE = False


def mx_kscale(k):
    if not WIDE:
        return np.ones(k)
    levels = np.array([10, -10, 5, -5, 0])
    if k % 512:
        return np.exp2(np.random.permutation(np.resize(levels, k // 32))).repeat(32)
    a = np.empty((k // 512, 16))
    for p in range(k // 512):
        a[p, :8] = np.random.permutation(np.resize(levels, 8))
        for g in range(8):
            far = levels[np.abs(levels - a[p, g]) >= 10]
            a[p, g + 8] = far[np.random.randint(len(far))]
    return np.exp2(a.ravel()).repeat(32)


def f64(x):
    return np.asarray(x).astype(np.float64)


def striped(idx):
    return np.tile(np.asarray(idx).reshape(-1, 16).T, (8, 1)).astype(np.uint16)


def unstriped(offs):
    return offs[:16].T.reshape(-1).astype(np.int64)


E2M1 = np.array([0.0, 0.5, 1.0, 1.5, 2.0, 3.0, 4.0, 6.0, -0.0, -0.5, -1.0, -1.5, -2.0, -3.0, -4.0, -6.0])


def pack_weight(w, fmt):
    k, n = w.shape
    w = f64(np.asarray(w, np.float32).astype(ml_dtypes.bfloat16)).reshape(k // 32, 32, n)
    amax = np.abs(w).max(1)
    if fmt == "e4m3":
        byte = np.frexp(amax)[1] - 1 + 127 - 7
    else:
        mant, ex = np.frexp(amax / 6.0)
        byte = np.where(mant > 0.5, ex, ex - 1) + 127
    byte = np.clip(np.where(amax > 0, byte, 1), 1, 254)
    scaled = (w * np.exp2(127.0 - byte)[:, None, :]).reshape(k, n).astype(np.float32)
    by_word = np.ascontiguousarray(scaled.reshape(k // 512, 128, 4, n).transpose(0, 1, 3, 2))
    if fmt == "e4m3":
        words = by_word.astype(ml_dtypes.float8_e4m3fn).view(np.uint8)
    else:
        c = by_word.astype(ml_dtypes.float4_e2m1fn).view(np.uint8) & 0xF
        words = (c[..., 0::2] | (c[..., 1::2] << 4)).reshape(k // 512, 128, 2 * n)
    return np.ascontiguousarray(words), np.ascontiguousarray(byte.astype(np.uint8).reshape(k // 512, 16, n))


def unpack_weight(words, scales, fmt):
    g, _, n = scales.shape
    words = np.ascontiguousarray(words).reshape(g, 128, n, -1)
    if fmt == "e4m3":
        vals = words.view(ml_dtypes.float8_e4m3fn).astype(np.float64)
    else:
        nib = np.empty((g, 128, n, 4), np.uint8)
        nib[..., 0::2] = words & 0xF
        nib[..., 1::2] = words >> 4
        vals = E2M1[nib]
    vals = vals * np.repeat(np.exp2(scales.astype(np.float64) - 127.0), 8, axis=1)[..., None]
    return vals.transpose(0, 1, 3, 2).reshape(g * 512, n)


def sigmoid(v):
    return 1.0 / (1.0 + np.exp(-v))


B, N, T, D, NQ = 1, 1024, 4096, 1024, 128
SEG = 32


def setup_inputs():
    n = np.random.standard_normal
    pages = np.random.permutation(T // 32)[:B * N // 32]
    idx = (pages[:, None] * 32 + np.arange(32)[None, :]).reshape(-1)
    s = mx_kscale(D)[:, None]
    kp = pack_weight(n((D, T)) / s, "e2m1")
    return {
        "qT": (n((B, D, NQ)) * s * (1.00 / np.sqrt(D))).astype(np.float32),
        "k_words": np.ascontiguousarray(kp[0].reshape(1, 2, 128, T, 2).transpose(0, 2, 3, 1, 4)).reshape(1, 128, T, 4),
        "k_scales": kp[1],
        "rk": np.tile(np.random.uniform(0.5, 1.0, 4096), (128, 1)).astype(np.float32),
        "offs": striped(idx),
    }


def reference(qT, k_words, k_scales, rk, offs):
    idx = unstriped(offs)
    pick = lambda x, which: x[:, which].reshape(x.shape[0], B, -1).transpose(1, 0, 2)
    k = unpack_weight(k_words.reshape(1, 128, T, 2, 2).transpose(0, 3, 1, 2, 4).reshape(2, 128, 2 * T), k_scales, "e2m1")
    kg = pick(k, idx)
    qq = mxq(f64(qT), 1, "e4m3")
    a = qq.transpose(0, 2, 1) @ kg
    y = sigmoid(6.0 * (a * pick(f64(rk), idx)[:, :1, :] - 1.0)).reshape(B, NQ, N // SEG, SEG).sum(-1)
    return y

@@ -1,0 +1,152 @@
+from contextlib import ExitStack
+
+import concourse.mybir as mybir
+from concourse.masks import make_identity
+
+F32 = mybir.dt.float32
+BF16 = mybir.dt.bfloat16
+I32 = mybir.dt.int32
+U32 = mybir.dt.uint32
+U16 = mybir.dt.uint16
+U8 = mybir.dt.uint8
+FP8X4 = mybir.dt.float8_e4m3fn_x4
+FP4X4 = mybir.dt.float4_e2m1fn_x4
+ACT = mybir.ActivationFunctionType
+
+P = 128
+T = 4096
+N = 1024
+NQ = 128
+PASSES = 2
+SEG = 32
+TILES = N // P
+FLOPS = 2 * 1024 * N * NQ
+
+
+def tile_attend_page_softcount_kernel(tc, qT, k_words, k_scales, rk, offs, out):
+    nc = tc.nc
+    with ExitStack() as ctx:
+        keep = ctx.enter_context(tc.tile_pool(name="keep", bufs=1))
+        score_pool = ctx.enter_context(tc.psum_pool(name="score", bufs=4))
+        turn_pool = ctx.enter_context(tc.psum_pool(name="turn", bufs=4))
+
+        offsets = keep.tile([P, N // 16], U16, name="offsets")
+        scale_pool = keep.tile([P, T], U8, name="scale_pool")
+        rk_pool = keep.tile([P, T], F32, name="rk_pool")
+        word_pool = keep.tile([P, T], I32, name="word_pool")
+        q_raw = [keep.tile([P, 4, NQ], F32, name=f"q_raw{o}") for o in range(PASSES)]
+
+        nc.sync.dma_start(offsets[:], offs)
+        nc.sync.dma_start(
+            scale_pool[0:32, :].bitcast(I32), k_scales.rearrange("o f t -> (o f) t").bitcast(I32)
+        )
+        nc.sync.dma_start(rk_pool[P - 1 : P, :], rk[0:1, :])
+        nc.sync.dma_start(word_pool[:], k_words[0].rearrange("p t b -> p (t b)").bitcast(I32))
+        for o in range(PASSES):
+            nc.sync.dma_start(
+                q_raw[o][:], qT[0, 512 * o : 512 * (o + 1), :].rearrange("(p j) w -> p j w", j=4)
+            )
+
+        planes = keep.tile([P, PASSES, N], U8, name="planes", align_bytes=64)
+        nc.vector.memset(scale_pool[32:64, :].bitcast(I32), 0)
+        nc.vector.memset(scale_pool[64:128, :].bitcast(I32), 0)
+        nc.vector.memset(planes[:].bitcast(I32), 0)
+        nc.vector.memset(rk_pool[0 : P - 1, 0 : T // 2], 0.0)
+        ident = keep.tile([P, P], F32, name="ident")
+        make_identity(nc, ident[:])
+
+        scale_rows = keep.tile([P, N], U8, name="scale_rows")
+        nc.vector.tensor_copy(scale_rows[:], scale_pool[:].indirect(offsets[:]))
+        nc.vector.memset(rk_pool[0 : P - 1, T // 2 : T], 0.0)
+        for o in range(PASSES):
+            for quad in range(4):
+                row = 16 * o + 4 * quad
+                queue = nc.gpsimd if (o == 1 and quad >= 2) else nc.scalar
+                queue.dma_start(
+                    planes[32 * quad : 32 * quad + 4, o, :].bitcast(I32),
+                    scale_rows[row : row + 4, :].bitcast(I32),
+                )
+
+        rk_slots = keep.tile([P, N], F32, name="rk_slots")
+        nc.vector.tensor_copy(rk_slots[:], rk_pool[:].indirect(offsets[:]))
+        rk6 = keep.tile([P, TILES], F32, name="rk6")
+        for h in range(2):
+            turned = turn_pool.tile([P, 4, P], F32, name="turned")
+            for i in range(4):
+                k = 4 * h + i
+                nc.tensor.transpose(turned[:, i, :], rk_slots[:, P * k : P * (k + 1)], ident[:])
+            nc.scalar.activation(rk6[:, 4 * h : 4 * h + 4], turned[:, :, P - 1], ACT.Copy, scale=6.0)
+
+        words = [keep.tile([P, N // 2], U32, name=f"words{h}") for h in range(2)]
+        for h in range(2):
+            nc.vector.tensor_copy(
+                words[h][:], word_pool[:].bitcast(U32).indirect(offsets[:, 32 * h : 32 * (h + 1)])
+            )
+
+        keys = keep.tile([P, PASSES, 2 * N], U8, name="keys", align_bytes=64)
+        q_bf = [keep.tile([P, NQ, 4], BF16, name=f"q_bf{o}", align_bytes=64) for o in range(PASSES)]
+        q_codes = [keep.tile([P, NQ], U32, name=f"q_codes{o}", align_bytes=64) for o in range(PASSES)]
+        q_scales = [keep.tile([P, NQ], U8, name=f"q_scales{o}", align_bytes=64) for o in range(PASSES)]
+
+        def split(piece):
+            h, c = divmod(piece, 2)
+            src = words[h][:, 256 * c : 256 * (c + 1)].bitcast(U16).rearrange("p (n o) -> p o n", o=2)
+            nc.vector.tensor_copy(keys[:].bitcast(U16)[:, :, 256 * piece : 256 * (piece + 1)], src)
+
+        def quantise(o):
+            nc.scalar.copy(q_bf[o][:], q_raw[o][:].rearrange("p j w -> p w j"))
+            nc.vector.quantize_mx(
+                out=q_codes[o][:].bitcast(FP8X4),
+                scales=q_scales[o][:],
+                in_=q_bf[o][:].rearrange("p w j -> p (w j)"),
+            )
+
+        split(0)
+        quantise(0)
+        split(1)
+        quantise(1)
+        split(2)
+        split(3)
+
+        match = keep.tile([P, N], F32, name="match")
+        counts = keep.tile([P, N // SEG], F32, name="counts")
+        scores = {}
+
+        def multiply(k, o):
+            if o == 0:
+                scores[k] = score_pool.tile([P, NQ], F32, name="scores")
+            nc.tensor.matmul_mx(
+                out=scores[k][:],
+                lhsT=keys[:, o, 2 * P * k : 2 * P * (k + 1)].bitcast(FP4X4),
+                lhsT_scale=planes[:, o, P * k : P * (k + 1)],
+                rhs=q_codes[o][:].bitcast(FP8X4),
+                rhs_scale=q_scales[o][:],
+                start=(o == 0),
+                stop=(o == PASSES - 1),
+            )
+            if o == PASSES - 1:
+                nc.scalar.activation(
+                    match[:, P * k : P * (k + 1)], scores[k][:], ACT.Sigmoid, bias=-6.0, scale=rk6[:, k : k + 1]
+                )
+
+        def count(first, last):
+            turned = turn_pool.tile([P, 4, P], F32, name="turned")
+            for k in range(first, last):
+                nc.tensor.transpose(turned[:, k - first, :], match[:, P * k : P * (k + 1)], ident[:])
+            nc.vector.tensor_reduce(
+                counts[:, 4 * first : 4 * last],
+                turned[:, 0 : last - first, :].rearrange("p k (j s) -> p (k j) s", s=SEG),
+                mybir.AxisListType.X,
+                mybir.AluOpType.add,
+            )
+
+        for o in range(PASSES):
+            for k in range(4):
+                multiply(k, o)
+        for k in range(4, TILES):
+            for o in range(PASSES):
+                multiply(k, o)
+        count(0, 4)
+        count(4, 6)
+        count(6, 8)
+        nc.sync.dma_start(out[0], counts[:])

@@ -28,17 +28,18 @@ def tile_attend_page_softcount_kernel(tc, qT, k_words, k_scales, rk, offs, out):
     with ExitStack() as ctx:
         keep = ctx.enter_context(tc.tile_pool(name="keep", bufs=1))
         score_pool = ctx.enter_context(tc.psum_pool(name="score", bufs=4))
-        turn_pool = ctx.enter_context(tc.psum_pool(name="turn", bufs=4))
+        turn_pool = ctx.enter_context(tc.psum_pool(name="turn", bufs=3))
+        warm_pool = ctx.enter_context(tc.psum_pool(name="warm", bufs=1))
 
         offsets = keep.tile([P, N // 16], U16, name="offsets")
-        scale_pool = keep.tile([P, T], U8, name="scale_pool")
+        scale_pool = keep.tile([P, T + 4], U8, name="scale_pool")
         rk_pool = keep.tile([P, T], F32, name="rk_pool")
         word_pool = keep.tile([P, T], I32, name="word_pool")
         q_raw = [keep.tile([P, 4, NQ], F32, name=f"q_raw{o}") for o in range(PASSES)]
 
         nc.sync.dma_start(offsets[:], offs)
         nc.sync.dma_start(
-            scale_pool[0:32, :].bitcast(I32), k_scales.rearrange("o f t -> (o f) t").bitcast(I32)
+            scale_pool[96:128, 0:T].bitcast(I32), k_scales.rearrange("o f t -> (o f) t").bitcast(I32)
         )
         nc.sync.dma_start(rk_pool[P - 1 : P, :], rk[0:1, :])
         nc.sync.dma_start(word_pool[:], k_words[0].rearrange("p t b -> p (t b)").bitcast(I32))
@@ -47,23 +48,25 @@ def tile_attend_page_softcount_kernel(tc, qT, k_words, k_scales, rk, offs, out):
                 q_raw[o][:], qT[0, 512 * o : 512 * (o + 1), :].rearrange("(p j) w -> p j w", j=4)
             )
 
-        planes = keep.tile([P, PASSES, N], U8, name="planes", align_bytes=64)
-        nc.vector.memset(scale_pool[32:64, :].bitcast(I32), 0)
-        nc.vector.memset(scale_pool[64:128, :].bitcast(I32), 0)
+        planes = keep.tile([P, PASSES * N + 4], U8, name="planes", align_bytes=64)
+        shift = keep.tile([P, 1], F32, name="shift")
+        nc.vector.memset(shift[:], -6.0)
+        nc.vector.memset(scale_pool[0:96, :].bitcast(I32), 0)
         nc.vector.memset(planes[:].bitcast(I32), 0)
-        nc.vector.memset(rk_pool[0 : P - 1, 0 : T // 2], 0.0)
         ident = keep.tile([P, P], F32, name="ident")
         make_identity(nc, ident[:])
+        nc.gpsimd.memset(rk_pool[0 : P - 1, :], 0.0)
+        table_warm = keep.tile([P, 1], F32, name="table_warm")
+        nc.scalar.activation(table_warm[:], shift[:], ACT.Sigmoid)
 
         scale_rows = keep.tile([P, N], U8, name="scale_rows")
-        nc.vector.tensor_copy(scale_rows[:], scale_pool[:].indirect(offsets[:]))
-        nc.vector.memset(rk_pool[0 : P - 1, T // 2 : T], 0.0)
+        nc.vector.tensor_copy(scale_rows[:], scale_pool[:, 0:T].indirect(offsets[:]))
         for o in range(PASSES):
             for quad in range(4):
-                row = 16 * o + 4 * quad
+                row = 96 + 16 * o + 4 * quad
                 queue = nc.gpsimd if (o == 1 and quad >= 2) else nc.scalar
                 queue.dma_start(
-                    planes[32 * quad : 32 * quad + 4, o, :].bitcast(I32),
+                    planes[32 * quad : 32 * quad + 4, N * o : N * (o + 1)].bitcast(I32),
                     scale_rows[row : row + 4, :].bitcast(I32),
                 )
 
@@ -77,21 +80,25 @@ def tile_attend_page_softcount_kernel(tc, qT, k_words, k_scales, rk, offs, out):
                 nc.tensor.transpose(turned[:, i, :], rk_slots[:, P * k : P * (k + 1)], ident[:])
             nc.scalar.activation(rk6[:, 4 * h : 4 * h + 4], turned[:, :, P - 1], ACT.Copy, scale=6.0)
 
-        words = [keep.tile([P, N // 2], U32, name=f"words{h}") for h in range(2)]
-        for h in range(2):
+        warm = warm_pool.tile([P, 4, P], F32, name="warm")
+        for i in range(10):
+            nc.tensor.transpose(warm[:, i % 4, :], rk_slots[:, 0:P], ident[:])
+
+        def gather_words(h):
+            words = keep.tile([P, N // 2], U32, name="words")
             nc.vector.tensor_copy(
-                words[h][:], word_pool[:].bitcast(U32).indirect(offsets[:, 32 * h : 32 * (h + 1)])
+                words[:], word_pool[:].bitcast(U32).indirect(offsets[:, 32 * h : 32 * (h + 1)])
             )
+            return words
 
         keys = keep.tile([P, PASSES, 2 * N], U8, name="keys", align_bytes=64)
         q_bf = [keep.tile([P, NQ, 4], BF16, name=f"q_bf{o}", align_bytes=64) for o in range(PASSES)]
         q_codes = [keep.tile([P, NQ], U32, name=f"q_codes{o}", align_bytes=64) for o in range(PASSES)]
         q_scales = [keep.tile([P, NQ], U8, name=f"q_scales{o}", align_bytes=64) for o in range(PASSES)]
 
-        def split(piece):
-            h, c = divmod(piece, 2)
-            src = words[h][:, 256 * c : 256 * (c + 1)].bitcast(U16).rearrange("p (n o) -> p o n", o=2)
-            nc.vector.tensor_copy(keys[:].bitcast(U16)[:, :, 256 * piece : 256 * (piece + 1)], src)
+        def split(words, first, last):
+            src = words[:, first % 512 : (last - 1) % 512 + 1].bitcast(U16).rearrange("p (n o) -> p o n", o=2)
+            nc.vector.tensor_copy(keys[:].bitcast(U16)[:, :, first:last], src)
 
         def quantise(o):
             nc.scalar.copy(q_bf[o][:], q_raw[o][:].rearrange("p j w -> p w j"))
@@ -101,12 +108,15 @@ def tile_attend_page_softcount_kernel(tc, qT, k_words, k_scales, rk, offs, out):
                 in_=q_bf[o][:].rearrange("p w j -> p (w j)"),
             )
 
-        split(0)
+        words = gather_words(0)
+        split(words, 0, 256)
         quantise(0)
-        split(1)
+        split(words, 256, 512)
         quantise(1)
-        split(2)
-        split(3)
+        words = gather_words(1)
+        split(words, 512, 768)
+        split(words, 768, 896)
+        split(words, 896, 1024)
 
         match = keep.tile([P, N], F32, name="match")
         counts = keep.tile([P, N // SEG], F32, name="counts")
@@ -118,7 +128,7 @@ def tile_attend_page_softcount_kernel(tc, qT, k_words, k_scales, rk, offs, out):
             nc.tensor.matmul_mx(
                 out=scores[k][:],
                 lhsT=keys[:, o, 2 * P * k : 2 * P * (k + 1)].bitcast(FP4X4),
-                lhsT_scale=planes[:, o, P * k : P * (k + 1)],
+                lhsT_scale=planes[:, N * o + P * k : N * o + P * (k + 1)],
                 rhs=q_codes[o][:].bitcast(FP8X4),
                 rhs_scale=q_scales[o][:],
                 start=(o == 0),
@@ -126,7 +136,7 @@ def tile_attend_page_softcount_kernel(tc, qT, k_words, k_scales, rk, offs, out):
             )
             if o == PASSES - 1:
                 nc.scalar.activation(
-                    match[:, P * k : P * (k + 1)], scores[k][:], ACT.Sigmoid, bias=-6.0, scale=rk6[:, k : k + 1]
+                    match[:, P * k : P * (k + 1)], scores[k][:], ACT.Sigmoid, bias=shift[:], scale=rk6[:, k : k + 1]
                 )
 
         def count(first, last):
@@ -143,10 +153,11 @@ def tile_attend_page_softcount_kernel(tc, qT, k_words, k_scales, rk, offs, out):
         for o in range(PASSES):
             for k in range(4):
                 multiply(k, o)
+        count(0, 4)
         for k in range(4, TILES):
             for o in range(PASSES):
                 multiply(k, o)
-        count(0, 4)
         count(4, 6)
-        count(6, 8)
+        count(6, 7)
+        count(7, 8)
         nc.sync.dma_start(out[0], counts[:])

@@ -28,47 +28,50 @@ def tile_attend_page_softcount_kernel(tc, qT, k_words, k_scales, rk, offs, out):
     with ExitStack() as ctx:
         keep = ctx.enter_context(tc.tile_pool(name="keep", bufs=1))
         score_pool = ctx.enter_context(tc.psum_pool(name="score", bufs=4))
-        turn_pool = ctx.enter_context(tc.psum_pool(name="turn", bufs=3))
-        warm_pool = ctx.enter_context(tc.psum_pool(name="warm", bufs=1))
+        turn_pool = ctx.enter_context(tc.psum_pool(name="turn", bufs=4))
 
         offsets = keep.tile([P, N // 16], U16, name="offsets")
-        scale_pool = keep.tile([P, T + 4], U8, name="scale_pool")
+        scale_pool = keep.tile([P, T], U8, name="scale_pool", tag="stage")
         rk_pool = keep.tile([P, T], F32, name="rk_pool")
         word_pool = keep.tile([P, T], I32, name="word_pool")
-        q_raw = [keep.tile([P, 4, NQ], F32, name=f"q_raw{o}") for o in range(PASSES)]
 
         nc.sync.dma_start(offsets[:], offs)
         nc.sync.dma_start(
-            scale_pool[96:128, 0:T].bitcast(I32), k_scales.rearrange("o f t -> (o f) t").bitcast(I32)
+            scale_pool[96:128, :].bitcast(I32), k_scales.rearrange("o f t -> (o f) t").bitcast(I32)
         )
         nc.sync.dma_start(rk_pool[P - 1 : P, :], rk[0:1, :])
         nc.sync.dma_start(word_pool[:], k_words[0].rearrange("p t b -> p (t b)").bitcast(I32))
-        for o in range(PASSES):
-            nc.sync.dma_start(
-                q_raw[o][:], qT[0, 512 * o : 512 * (o + 1), :].rearrange("(p j) w -> p j w", j=4)
-            )
 
-        planes = keep.tile([P, PASSES * N + 4], U8, name="planes", align_bytes=64)
+        planes = keep.tile([P, PASSES * N], U8, name="planes", align_bytes=64)
         shift = keep.tile([P, 1], F32, name="shift")
         nc.vector.memset(shift[:], -6.0)
         nc.vector.memset(scale_pool[0:96, :].bitcast(I32), 0)
         nc.vector.memset(planes[:].bitcast(I32), 0)
+        nc.vector.memset(rk_pool[0 : P - 1, 0 : T // 2], 0.0)
         ident = keep.tile([P, P], F32, name="ident")
         make_identity(nc, ident[:])
-        nc.gpsimd.memset(rk_pool[0 : P - 1, :], 0.0)
         table_warm = keep.tile([P, 1], F32, name="table_warm")
         nc.scalar.activation(table_warm[:], shift[:], ACT.Sigmoid)
 
         scale_rows = keep.tile([P, N], U8, name="scale_rows")
-        nc.vector.tensor_copy(scale_rows[:], scale_pool[:, 0:T].indirect(offsets[:]))
-        for o in range(PASSES):
+        nc.vector.tensor_copy(scale_rows[:], scale_pool[:].indirect(offsets[:]))
+        nc.vector.memset(rk_pool[0 : P - 1, T // 2 : T], 0.0)
+
+        def place_scales(o):
             for quad in range(4):
                 row = 96 + 16 * o + 4 * quad
-                queue = nc.gpsimd if (o == 1 and quad >= 2) else nc.scalar
-                queue.dma_start(
+                nc.sync.dma_start(
                     planes[32 * quad : 32 * quad + 4, N * o : N * (o + 1)].bitcast(I32),
                     scale_rows[row : row + 4, :].bitcast(I32),
                 )
+
+        place_scales(0)
+        q_raw = keep.tile([P, PASSES, 4, NQ], F32, name="q_raw", tag="stage")
+        for o in range(PASSES):
+            nc.sync.dma_start(
+                q_raw[:, o, :, :], qT[0, 512 * o : 512 * (o + 1), :].rearrange("(p j) w -> p j w", j=4)
+            )
+        place_scales(1)
 
         rk_slots = keep.tile([P, N], F32, name="rk_slots")
         nc.vector.tensor_copy(rk_slots[:], rk_pool[:].indirect(offsets[:]))
@@ -80,9 +83,6 @@ def tile_attend_page_softcount_kernel(tc, qT, k_words, k_scales, rk, offs, out):
                 nc.tensor.transpose(turned[:, i, :], rk_slots[:, P * k : P * (k + 1)], ident[:])
             nc.scalar.activation(rk6[:, 4 * h : 4 * h + 4], turned[:, :, P - 1], ACT.Copy, scale=6.0)
 
-        warm = warm_pool.tile([P, 4, P], F32, name="warm")
-        for i in range(10):
-            nc.tensor.transpose(warm[:, i % 4, :], rk_slots[:, 0:P], ident[:])
 
         def gather_words(h):
             words = keep.tile([P, N // 2], U32, name="words")
@@ -101,7 +101,7 @@ def tile_attend_page_softcount_kernel(tc, qT, k_words, k_scales, rk, offs, out):
             nc.vector.tensor_copy(keys[:].bitcast(U16)[:, :, first:last], src)
 
         def quantise(o):
-            nc.scalar.copy(q_bf[o][:], q_raw[o][:].rearrange("p j w -> p w j"))
+            nc.scalar.copy(q_bf[o][:], q_raw[:, o, :, :].rearrange("p j w -> p w j"))
             nc.vector.quantize_mx(
                 out=q_codes[o][:].bitcast(FP8X4),
                 scales=q_scales[o][:],

@@ -20,6 +20,8 @@ NQ = 128
 PASSES = 2
 SEG = 32
 TILES = N // P
+ZEROED = 2048
+FILL = 64
 FLOPS = 2 * 1024 * N * NQ
 
 
@@ -32,13 +34,15 @@ def tile_attend_page_softcount_kernel(tc, qT, k_words, k_scales, rk, offs, out):
 
         offsets = keep.tile([P, N // 16], U16, name="offsets")
         scale_pool = keep.tile([P, T], U8, name="scale_pool", tag="stage")
-        rk_pool = keep.tile([P, T], F32, name="rk_pool")
+        rk_pool = keep.tile([P, T], F32, name="rk_pool", tag="lookup", align_bytes=64)
         word_pool = keep.tile([P, T], I32, name="word_pool")
 
         nc.sync.dma_start(offsets[:], offs)
         nc.sync.dma_start(
             scale_pool[96:128, :].bitcast(I32), k_scales.rearrange("o f t -> (o f) t").bitcast(I32)
         )
+        rk_fill = keep.tile([P, FILL], F32, name="rk_fill")
+        nc.sync.dma_start(rk_fill[:], rk[:, 0:FILL])
         nc.sync.dma_start(rk_pool[P - 1 : P, :], rk[0:1, :])
         nc.sync.dma_start(word_pool[:], k_words[0].rearrange("p t b -> p (t b)").bitcast(I32))
 
@@ -47,15 +51,20 @@ def tile_attend_page_softcount_kernel(tc, qT, k_words, k_scales, rk, offs, out):
         nc.vector.memset(shift[:], -6.0)
         nc.vector.memset(scale_pool[0:96, :].bitcast(I32), 0)
         nc.vector.memset(planes[:].bitcast(I32), 0)
-        nc.vector.memset(rk_pool[0 : P - 1, 0 : T // 2], 0.0)
+        nc.vector.memset(rk_pool[0 : P - 1, 0:ZEROED], 0.0)
         ident = keep.tile([P, P], F32, name="ident")
         make_identity(nc, ident[:])
         table_warm = keep.tile([P, 1], F32, name="table_warm")
         nc.scalar.activation(table_warm[:], shift[:], ACT.Sigmoid)
+        repeats = (T - ZEROED) // FILL
+        nc.scalar.activation(
+            rk_pool[0 : P - 1, ZEROED:T].rearrange("p (r c) -> p r c", c=FILL),
+            rk_fill[0 : P - 1, :].unsqueeze(1).to_broadcast([P - 1, repeats, FILL]),
+            ACT.Copy,
+        )
 
         scale_rows = keep.tile([P, N], U8, name="scale_rows")
         nc.vector.tensor_copy(scale_rows[:], scale_pool[:].indirect(offsets[:]))
-        nc.vector.memset(rk_pool[0 : P - 1, T // 2 : T], 0.0)
 
         def place_scales(o):
             for quad in range(4):
@@ -75,24 +84,16 @@ def tile_attend_page_softcount_kernel(tc, qT, k_words, k_scales, rk, offs, out):
 
         rk_slots = keep.tile([P, N], F32, name="rk_slots")
         nc.vector.tensor_copy(rk_slots[:], rk_pool[:].indirect(offsets[:]))
-        rk6 = keep.tile([P, TILES], F32, name="rk6")
-        for h in range(2):
-            turned = turn_pool.tile([P, 4, P], F32, name="turned")
-            for i in range(4):
-                k = 4 * h + i
-                nc.tensor.transpose(turned[:, i, :], rk_slots[:, P * k : P * (k + 1)], ident[:])
-            nc.scalar.activation(rk6[:, 4 * h : 4 * h + 4], turned[:, :, P - 1], ACT.Copy, scale=6.0)
 
-
-        def gather_words(h):
-            words = keep.tile([P, N // 2], U32, name="words")
+        def gather_words(h, slot):
+            words = keep.tile([P, N // 2], U32, name=f"words{h}", tag=slot, align_bytes=64)
             nc.vector.tensor_copy(
                 words[:], word_pool[:].bitcast(U32).indirect(offsets[:, 32 * h : 32 * (h + 1)])
             )
             return words
 
         keys = keep.tile([P, PASSES, 2 * N], U8, name="keys", align_bytes=64)
-        q_bf = [keep.tile([P, NQ, 4], BF16, name=f"q_bf{o}", align_bytes=64) for o in range(PASSES)]
+        q_bf = keep.tile([P, PASSES, NQ, 4], BF16, name="q_bf", tag="late", align_bytes=64)
         q_codes = [keep.tile([P, NQ], U32, name=f"q_codes{o}", align_bytes=64) for o in range(PASSES)]
         q_scales = [keep.tile([P, NQ], U8, name=f"q_scales{o}", align_bytes=64) for o in range(PASSES)]
 
@@ -101,22 +102,30 @@ def tile_attend_page_softcount_kernel(tc, qT, k_words, k_scales, rk, offs, out):
             nc.vector.tensor_copy(keys[:].bitcast(U16)[:, :, first:last], src)
 
         def quantise(o):
-            nc.scalar.copy(q_bf[o][:], q_raw[:, o, :, :].rearrange("p j w -> p w j"))
+            nc.scalar.copy(q_bf[:, o, :, :], q_raw[:, o, :, :].rearrange("p j w -> p w j"))
             nc.vector.quantize_mx(
                 out=q_codes[o][:].bitcast(FP8X4),
                 scales=q_scales[o][:],
-                in_=q_bf[o][:].rearrange("p w j -> p (w j)"),
+                in_=q_bf[:, o, :, :].rearrange("p w j -> p (w j)"),
             )
 
-        words = gather_words(0)
+        words = gather_words(0, "lookup")
         split(words, 0, 256)
         quantise(0)
         split(words, 256, 512)
         quantise(1)
-        words = gather_words(1)
-        split(words, 512, 768)
-        split(words, 768, 896)
-        split(words, 896, 1024)
+        rk6 = keep.tile([P, TILES], F32, name="rk6", tag="stage")
+        for h in range(2):
+            turned = turn_pool.tile([P, 4, P], F32, name="turned")
+            for i in range(4):
+                k = 4 * h + i
+                nc.tensor.transpose(turned[:, i, :], rk_slots[:, P * k : P * (k + 1)], ident[:])
+            nc.scalar.activation(rk6[:, 4 * h : 4 * h + 4], turned[:, :, P - 1], ACT.Copy, scale=6.0)
+
+        words = gather_words(1, "late")
+        split(words, 512, 640)
+        split(words, 640, 768)
+        split(words, 768, 1024)
 
         match = keep.tile([P, N], F32, name="match")
         counts = keep.tile([P, N // SEG], F32, name="counts")

@@ -20,8 +20,10 @@ NQ = 128
 PASSES = 2
 SEG = 32
 TILES = N // P
-ZEROED = 2048
-FILL = 64
+HALF = N // 2
+RUN = 8
+BANK = 512
+ZERO_EARLY = 2048
 FLOPS = 2 * 1024 * N * NQ
 
 
@@ -29,21 +31,25 @@ def tile_attend_page_softcount_kernel(tc, qT, k_words, k_scales, rk, offs, out):
     nc = tc.nc
     with ExitStack() as ctx:
         keep = ctx.enter_context(tc.tile_pool(name="keep", bufs=1))
-        score_pool = ctx.enter_context(tc.psum_pool(name="score", bufs=4))
-        turn_pool = ctx.enter_context(tc.psum_pool(name="turn", bufs=4))
+        psum = ctx.enter_context(tc.psum_pool(name="psum", bufs=1))
+
+        def in_bank(bank, name, banks=1):
+            return psum.tile([P, banks * BANK], F32, name=name, offset=4 * BANK * bank)
 
         offsets = keep.tile([P, N // 16], U16, name="offsets")
-        scale_pool = keep.tile([P, T], U8, name="scale_pool", tag="stage")
+        scale_pool = keep.tile([P, T], U8, name="scale_pool")
         rk_pool = keep.tile([P, T], F32, name="rk_pool", tag="lookup", align_bytes=64)
         word_pool = keep.tile([P, T], I32, name="word_pool")
+        q_raw = keep.tile([P, PASSES, 4, NQ], F32, name="q_raw", tag="dealt0")
 
         nc.sync.dma_start(offsets[:], offs)
         nc.sync.dma_start(
             scale_pool[96:128, :].bitcast(I32), k_scales.rearrange("o f t -> (o f) t").bitcast(I32)
         )
-        rk_fill = keep.tile([P, FILL], F32, name="rk_fill")
-        nc.sync.dma_start(rk_fill[:], rk[:, 0:FILL])
         nc.sync.dma_start(rk_pool[P - 1 : P, :], rk[0:1, :])
+        nc.sync.dma_start(
+            q_raw[:].rearrange("p o j w -> p o (j w)"), qT[0].rearrange("(o p j) w -> p o (j w)", o=PASSES, j=4)
+        )
         nc.sync.dma_start(word_pool[:], k_words[0].rearrange("p t b -> p (t b)").bitcast(I32))
 
         planes = keep.tile([P, PASSES * N], U8, name="planes", align_bytes=64)
@@ -51,122 +57,111 @@ def tile_attend_page_softcount_kernel(tc, qT, k_words, k_scales, rk, offs, out):
         nc.vector.memset(shift[:], -6.0)
         nc.vector.memset(scale_pool[0:96, :].bitcast(I32), 0)
         nc.vector.memset(planes[:].bitcast(I32), 0)
-        nc.vector.memset(rk_pool[0 : P - 1, 0:ZEROED], 0.0)
         ident = keep.tile([P, P], F32, name="ident")
         make_identity(nc, ident[:])
         table_warm = keep.tile([P, 1], F32, name="table_warm")
         nc.scalar.activation(table_warm[:], shift[:], ACT.Sigmoid)
-        repeats = (T - ZEROED) // FILL
-        nc.scalar.activation(
-            rk_pool[0 : P - 1, ZEROED:T].rearrange("p (r c) -> p r c", c=FILL),
-            rk_fill[0 : P - 1, :].unsqueeze(1).to_broadcast([P - 1, repeats, FILL]),
-            ACT.Copy,
-        )
 
         scale_rows = keep.tile([P, N], U8, name="scale_rows")
+        nc.vector.memset(rk_pool[0 : P - 1, 0:ZERO_EARLY].bitcast(I32), 0)
         nc.vector.tensor_copy(scale_rows[:], scale_pool[:].indirect(offsets[:]))
+        nc.vector.memset(rk_pool[0 : P - 1, ZERO_EARLY:T].bitcast(I32), 0)
+        scale_dealt = keep.tile([P, N], U8, name="scale_dealt")
+        nc.vector.tensor_copy(
+            scale_dealt[:].bitcast(I32).rearrange("p (h k j w) -> p h k j w", h=2, k=4, w=2),
+            scale_rows[:].bitcast(I32).rearrange("p (h j k w) -> p h k j w", h=2, k=4, w=2),
+        )
 
-        def place_scales(o):
+        for o in range(PASSES):
             for quad in range(4):
                 row = 96 + 16 * o + 4 * quad
                 nc.sync.dma_start(
                     planes[32 * quad : 32 * quad + 4, N * o : N * (o + 1)].bitcast(I32),
-                    scale_rows[row : row + 4, :].bitcast(I32),
+                    scale_dealt[row : row + 4, :].bitcast(I32),
                 )
 
-        place_scales(0)
-        q_raw = keep.tile([P, PASSES, 4, NQ], F32, name="q_raw", tag="stage")
+        q_bf = keep.tile([P, PASSES, NQ, 4], BF16, name="q_bf", tag="late1", align_bytes=64)
+        q_codes = keep.tile([P, PASSES * NQ], U32, name="q_codes", align_bytes=64)
+        q_scales = keep.tile([P, PASSES * NQ], U8, name="q_scales", align_bytes=64)
         for o in range(PASSES):
-            nc.sync.dma_start(
-                q_raw[:, o, :, :], qT[0, 512 * o : 512 * (o + 1), :].rearrange("(p j) w -> p j w", j=4)
+            nc.scalar.copy(q_bf[:, o, :, :], q_raw[:, o, :, :].rearrange("p j w -> p w j"))
+        nc.vector.quantize_mx(
+            out=q_codes[:].bitcast(FP8X4), scales=q_scales[:], in_=q_bf[:].rearrange("p o w j -> p (o w j)")
+        )
+
+        rk6 = keep.tile([P, TILES], F32, name="rk6")
+        for h in range(2):
+            rk_slots = keep.tile([P, HALF], F32, name=f"rk_slots{h}", tag=f"late{h}", align_bytes=64)
+            nc.vector.tensor_copy(rk_slots[:], rk_pool[:].indirect(offsets[:, 32 * h : 32 * (h + 1)]))
+            rk_dealt = keep.tile([P, 4, P], F32, name=f"rk_dealt{h}", tag=f"dealt{h}")
+            nc.scalar.activation(
+                rk_dealt[:].rearrange("p k (j s) -> p k j s", s=RUN),
+                rk_slots[:].rearrange("p (j k s) -> p k j s", k=4, s=RUN),
+                ACT.Copy,
+                scale=6.0,
             )
-        place_scales(1)
+            turned = in_bank(3 + 4 * h, f"turned{h}")[:].rearrange("p (k m) -> p k m", m=P)
+            for i in range(4):
+                nc.tensor.transpose(turned[:, i, :], rk_dealt[:, i, :], ident[:])
+            nc.scalar.copy(rk6[:, 4 * h : 4 * h + 4], turned[:, :, P - 1])
 
-        rk_slots = keep.tile([P, N], F32, name="rk_slots")
-        nc.vector.tensor_copy(rk_slots[:], rk_pool[:].indirect(offsets[:]))
+        keys = keep.tile([P, PASSES, 2 * N], U8, name="keys", align_bytes=64)
 
-        def gather_words(h, slot):
-            words = keep.tile([P, N // 2], U32, name=f"words{h}", tag=slot, align_bytes=64)
+        def gather_words(h):
+            words = keep.tile([P, HALF], U32, name=f"words{h}", tag="lookup", align_bytes=64)
             nc.vector.tensor_copy(
                 words[:], word_pool[:].bitcast(U32).indirect(offsets[:, 32 * h : 32 * (h + 1)])
             )
             return words
 
-        keys = keep.tile([P, PASSES, 2 * N], U8, name="keys", align_bytes=64)
-        q_bf = keep.tile([P, PASSES, NQ, 4], BF16, name="q_bf", tag="late", align_bytes=64)
-        q_codes = [keep.tile([P, NQ], U32, name=f"q_codes{o}", align_bytes=64) for o in range(PASSES)]
-        q_scales = [keep.tile([P, NQ], U8, name=f"q_scales{o}", align_bytes=64) for o in range(PASSES)]
-
         def split(words, first, last):
-            src = words[:, first % 512 : (last - 1) % 512 + 1].bitcast(U16).rearrange("p (n o) -> p o n", o=2)
-            nc.vector.tensor_copy(keys[:].bitcast(U16)[:, :, first:last], src)
-
-        def quantise(o):
-            nc.scalar.copy(q_bf[:, o, :, :], q_raw[:, o, :, :].rearrange("p j w -> p w j"))
-            nc.vector.quantize_mx(
-                out=q_codes[o][:].bitcast(FP8X4),
-                scales=q_scales[o][:],
-                in_=q_bf[:, o, :, :].rearrange("p w j -> p (w j)"),
-            )
-
-        words = gather_words(0, "lookup")
-        split(words, 0, 256)
-        quantise(0)
-        split(words, 256, 512)
-        quantise(1)
-        rk6 = keep.tile([P, TILES], F32, name="rk6", tag="stage")
-        for h in range(2):
-            turned = turn_pool.tile([P, 4, P], F32, name="turned")
-            for i in range(4):
-                k = 4 * h + i
-                nc.tensor.transpose(turned[:, i, :], rk_slots[:, P * k : P * (k + 1)], ident[:])
-            nc.scalar.activation(rk6[:, 4 * h : 4 * h + 4], turned[:, :, P - 1], ACT.Copy, scale=6.0)
-
-        words = gather_words(1, "late")
-        split(words, 512, 640)
-        split(words, 640, 768)
-        split(words, 768, 1024)
+            src = words[:].bitcast(U16).rearrange("p (j k s o) -> p o k j s", k=4, s=RUN, o=PASSES)
+            dst = keys[:].bitcast(U16).rearrange("p o (k j s) -> p o k j s", k=TILES, s=RUN)
+            nc.vector.tensor_copy(dst[:, :, first:last], src[:, :, first % 4 : (last - 1) % 4 + 1])
 
         match = keep.tile([P, N], F32, name="match")
         counts = keep.tile([P, N // SEG], F32, name="counts")
-        scores = {}
 
-        def multiply(k, o):
-            if o == 0:
-                scores[k] = score_pool.tile([P, NQ], F32, name="scores")
-            nc.tensor.matmul_mx(
-                out=scores[k][:],
-                lhsT=keys[:, o, 2 * P * k : 2 * P * (k + 1)].bitcast(FP4X4),
-                lhsT_scale=planes[:, N * o + P * k : N * o + P * (k + 1)],
-                rhs=q_codes[o][:].bitcast(FP8X4),
-                rhs_scale=q_scales[o][:],
-                start=(o == 0),
-                stop=(o == PASSES - 1),
-            )
-            if o == PASSES - 1:
-                nc.scalar.activation(
-                    match[:, P * k : P * (k + 1)], scores[k][:], ACT.Sigmoid, bias=shift[:], scale=rk6[:, k : k + 1]
+        def score(k):
+            if k == 3:
+                scores = in_bank(4, "scores3", banks=4)[:, 0:NQ]
+            else:
+                scores = in_bank(k, f"scores{k}")[:, 0:NQ]
+            for o in range(PASSES):
+                nc.tensor.matmul_mx(
+                    out=scores,
+                    lhsT=keys[:, o, 2 * P * k : 2 * P * (k + 1)].bitcast(FP4X4),
+                    lhsT_scale=planes[:, N * o + P * k : N * o + P * (k + 1)],
+                    rhs=q_codes[:, NQ * o : NQ * (o + 1)].bitcast(FP8X4),
+                    rhs_scale=q_scales[:, NQ * o : NQ * (o + 1)],
+                    start=(o == 0),
+                    stop=(o == PASSES - 1),
                 )
+            nc.scalar.activation(
+                match[:, P * k : P * (k + 1)], scores, ACT.Sigmoid, bias=shift[:], scale=rk6[:, k : k + 1]
+            )
 
-        def count(first, last):
-            turned = turn_pool.tile([P, 4, P], F32, name="turned")
-            for k in range(first, last):
-                nc.tensor.transpose(turned[:, k - first, :], match[:, P * k : P * (k + 1)], ident[:])
+        def count(h):
+            summed = in_bank(3 - 3 * h, f"summed{h}")[:, 0:P]
+            for i in range(4):
+                k = 4 * h + i
+                nc.tensor.matmul(
+                    summed, match[:, P * k : P * (k + 1)], ident[:], start=(i == 0), stop=(i == 3), is_transpose=True
+                )
             nc.vector.tensor_reduce(
-                counts[:, 4 * first : 4 * last],
-                turned[:, 0 : last - first, :].rearrange("p k (j s) -> p (k j) s", s=SEG),
+                counts[:, 16 * h : 16 * (h + 1)],
+                summed.rearrange("p (j s) -> p j s", s=RUN),
                 mybir.AxisListType.X,
                 mybir.AluOpType.add,
             )
 
-        for o in range(PASSES):
-            for k in range(4):
-                multiply(k, o)
-        count(0, 4)
-        for k in range(4, TILES):
-            for o in range(PASSES):
-                multiply(k, o)
-        count(4, 6)
-        count(6, 7)
-        count(7, 8)
+        for h in range(2):
+            words = gather_words(h)
+            split(words, 4 * h, 4 * h + 1)
+            split(words, 4 * h + 1, 4 * h + 2)
+            split(words, 4 * h + 2, 4 * h + 4)
+        for h in range(2):
+            for k in range(4 * h, 4 * h + 4):
+                score(k)
+            count(h)
         nc.sync.dma_start(out[0], counts[:])

@@ -23,7 +23,9 @@ TILES = N // P
 HALF = N // 2
 RUN = 8
 BANK = 512
-ZERO_EARLY = 2048
+HEAD = 64
+FILLED = 2048
+ZERO_EARLY = 3584
 FLOPS = 2 * 1024 * N * NQ
 
 
@@ -46,7 +48,9 @@ def tile_attend_page_softcount_kernel(tc, qT, k_words, k_scales, rk, offs, out):
         nc.sync.dma_start(
             scale_pool[96:128, :].bitcast(I32), k_scales.rearrange("o f t -> (o f) t").bitcast(I32)
         )
-        nc.sync.dma_start(rk_pool[P - 1 : P, :], rk[0:1, :])
+        rk_head = keep.tile([P, HEAD], F32, name="rk_head")
+        nc.sync.dma_start(rk_head[:], rk[:, 0:HEAD])
+        nc.sync.dma_start(rk_pool[P - 1 : P, HEAD:T], rk[0:1, HEAD:T])
         nc.sync.dma_start(
             q_raw[:].rearrange("p o j w -> p o (j w)"), qT[0].rearrange("(o p j) w -> p o (j w)", o=PASSES, j=4)
         )
@@ -62,8 +66,14 @@ def tile_attend_page_softcount_kernel(tc, qT, k_words, k_scales, rk, offs, out):
         table_warm = keep.tile([P, 1], F32, name="table_warm")
         nc.scalar.activation(table_warm[:], shift[:], ACT.Sigmoid)
 
+        nc.scalar.activation(rk_pool[:, 0:HEAD], rk_head[:], ACT.Copy)
+        nc.scalar.activation(
+            rk_pool[0 : P - 1, HEAD:FILLED].rearrange("p (r c) -> p r c", c=HEAD),
+            rk_head[0 : P - 1, :].unsqueeze(1).to_broadcast([P - 1, FILLED // HEAD - 1, HEAD]),
+            ACT.Copy,
+        )
         scale_rows = keep.tile([P, N], U8, name="scale_rows")
-        nc.vector.memset(rk_pool[0 : P - 1, 0:ZERO_EARLY].bitcast(I32), 0)
+        nc.vector.memset(rk_pool[0 : P - 1, FILLED:ZERO_EARLY].bitcast(I32), 0)
         nc.vector.tensor_copy(scale_rows[:], scale_pool[:].indirect(offsets[:]))
         nc.vector.memset(rk_pool[0 : P - 1, ZERO_EARLY:T].bitcast(I32), 0)
         scale_dealt = keep.tile([P, N], U8, name="scale_dealt")
@@ -80,42 +90,39 @@ def tile_attend_page_softcount_kernel(tc, qT, k_words, k_scales, rk, offs, out):
                     scale_dealt[row : row + 4, :].bitcast(I32),
                 )
 
-        q_bf = keep.tile([P, PASSES, NQ, 4], BF16, name="q_bf", tag="late1", align_bytes=64)
-        q_codes = keep.tile([P, PASSES * NQ], U32, name="q_codes", align_bytes=64)
+        q_bf = keep.tile([P, PASSES, NQ, 4], BF16, name="q_bf", tag="words1", align_bytes=64)
         q_scales = keep.tile([P, PASSES * NQ], U8, name="q_scales", align_bytes=64)
         for o in range(PASSES):
             nc.scalar.copy(q_bf[:, o, :, :], q_raw[:, o, :, :].rearrange("p j w -> p w j"))
-        nc.vector.quantize_mx(
-            out=q_codes[:].bitcast(FP8X4), scales=q_scales[:], in_=q_bf[:].rearrange("p o w j -> p (o w j)")
-        )
 
         rk6 = keep.tile([P, TILES], F32, name="rk6")
+        rk_dealt = keep.tile([P, N], F32, name="rk_dealt", tag="dealt0")
         for h in range(2):
-            rk_slots = keep.tile([P, HALF], F32, name=f"rk_slots{h}", tag=f"late{h}", align_bytes=64)
+            rk_slots = keep.tile([P, HALF], F32, name=f"rk_slots{h}", tag=f"words{2 * h}", align_bytes=64)
             nc.vector.tensor_copy(rk_slots[:], rk_pool[:].indirect(offsets[:, 32 * h : 32 * (h + 1)]))
-            rk_dealt = keep.tile([P, 4, P], F32, name=f"rk_dealt{h}", tag=f"dealt{h}")
             nc.scalar.activation(
-                rk_dealt[:].rearrange("p k (j s) -> p k j s", s=RUN),
+                rk_dealt[:, HALF * h : HALF * (h + 1)].rearrange("p (k j s) -> p k j s", k=4, s=RUN),
                 rk_slots[:].rearrange("p (j k s) -> p k j s", k=4, s=RUN),
                 ACT.Copy,
                 scale=6.0,
             )
             turned = in_bank(3 + 4 * h, f"turned{h}")[:].rearrange("p (k m) -> p k m", m=P)
             for i in range(4):
-                nc.tensor.transpose(turned[:, i, :], rk_dealt[:, i, :], ident[:])
+                nc.tensor.transpose(turned[:, i, :], rk_dealt[:, HALF * h + P * i : HALF * h + P * (i + 1)], ident[:])
             nc.scalar.copy(rk6[:, 4 * h : 4 * h + 4], turned[:, :, P - 1])
 
         keys = keep.tile([P, PASSES, 2 * N], U8, name="keys", align_bytes=64)
 
+        gathered = keep.tile([P, N - RUN], U32, name="gathered", tag="words0", align_bytes=64)
+
         def gather_words(h):
-            words = keep.tile([P, HALF], U32, name=f"words{h}", tag="lookup", align_bytes=64)
-            nc.vector.tensor_copy(
-                words[:], word_pool[:].bitcast(U32).indirect(offsets[:, 32 * h : 32 * (h + 1)])
-            )
+            first = (1 - h) * (HALF - RUN)
+            words = gathered[:, first : first + HALF]
+            nc.vector.tensor_copy(words, word_pool[:].bitcast(U32).indirect(offsets[:, 32 * h : 32 * (h + 1)]))
             return words
 
         def split(words, first, last):
-            src = words[:].bitcast(U16).rearrange("p (j k s o) -> p o k j s", k=4, s=RUN, o=PASSES)
+            src = words.bitcast(U16).rearrange("p (j k s o) -> p o k j s", k=4, s=RUN, o=PASSES)
             dst = keys[:].bitcast(U16).rearrange("p o (k j s) -> p o k j s", k=TILES, s=RUN)
             nc.vector.tensor_copy(dst[:, :, first:last], src[:, :, first % 4 : (last - 1) % 4 + 1])
 
@@ -155,8 +162,13 @@ def tile_attend_page_softcount_kernel(tc, qT, k_words, k_scales, rk, offs, out):
                 mybir.AluOpType.add,
             )
 
+        q_codes = keep.tile([P, PASSES * NQ], U32, name="q_codes", tag="lookup", align_bytes=64)
         for h in range(2):
             words = gather_words(h)
+            if h == 0:
+                nc.vector.quantize_mx(
+                    out=q_codes[:].bitcast(FP8X4), scales=q_scales[:], in_=q_bf[:].rearrange("p o w j -> p (o w j)")
+                )
             split(words, 4 * h, 4 * h + 1)
             split(words, 4 * h + 1, 4 * h + 2)
             split(words, 4 * h + 2, 4 * h + 4)

@@ -25,7 +25,7 @@ RUN = 8
 BANK = 512
 HEAD = 64
 FILLED = 2048
-ZERO_EARLY = 3584
+ZERO_EARLY = 3072
 FLOPS = 2 * 1024 * N * NQ
 
 
@@ -46,7 +46,7 @@ def tile_attend_page_softcount_kernel(tc, qT, k_words, k_scales, rk, offs, out):
 
         nc.sync.dma_start(offsets[:], offs)
         nc.sync.dma_start(
-            scale_pool[96:128, :].bitcast(I32), k_scales.rearrange("o f t -> (o f) t").bitcast(I32)
+            scale_pool[0:32, :].bitcast(I32), k_scales.rearrange("o f t -> (o f) t").bitcast(I32)
         )
         rk_head = keep.tile([P, HEAD], F32, name="rk_head")
         nc.sync.dma_start(rk_head[:], rk[:, 0:HEAD])
@@ -56,11 +56,12 @@ def tile_attend_page_softcount_kernel(tc, qT, k_words, k_scales, rk, offs, out):
         )
         nc.sync.dma_start(word_pool[:], k_words[0].rearrange("p t b -> p (t b)").bitcast(I32))
 
-        planes = keep.tile([P, PASSES * N], U8, name="planes", align_bytes=64)
+        planes = [keep.tile([P, N], U8, name=f"plane{o}", align_bytes=64) for o in range(PASSES)]
         shift = keep.tile([P, 1], F32, name="shift")
         nc.vector.memset(shift[:], -6.0)
-        nc.vector.memset(scale_pool[0:96, :].bitcast(I32), 0)
-        nc.vector.memset(planes[:].bitcast(I32), 0)
+        nc.vector.memset(scale_pool[32:64, :].bitcast(I32), 0)
+        nc.vector.memset(scale_pool[64:128, :].bitcast(I32), 0)
+        nc.vector.memset(planes[1][:].bitcast(I32), 0)
         ident = keep.tile([P, P], F32, name="ident")
         make_identity(nc, ident[:])
         table_warm = keep.tile([P, 1], F32, name="table_warm")
@@ -76,18 +77,16 @@ def tile_attend_page_softcount_kernel(tc, qT, k_words, k_scales, rk, offs, out):
         nc.vector.memset(rk_pool[0 : P - 1, FILLED:ZERO_EARLY].bitcast(I32), 0)
         nc.vector.tensor_copy(scale_rows[:], scale_pool[:].indirect(offsets[:]))
         nc.vector.memset(rk_pool[0 : P - 1, ZERO_EARLY:T].bitcast(I32), 0)
-        scale_dealt = keep.tile([P, N], U8, name="scale_dealt")
         nc.vector.tensor_copy(
-            scale_dealt[:].bitcast(I32).rearrange("p (h k j w) -> p h k j w", h=2, k=4, w=2),
+            planes[0][:].bitcast(I32).rearrange("p (h k j w) -> p h k j w", h=2, k=4, w=2),
             scale_rows[:].bitcast(I32).rearrange("p (h j k w) -> p h k j w", h=2, k=4, w=2),
         )
 
         for o in range(PASSES):
-            for quad in range(4):
-                row = 96 + 16 * o + 4 * quad
+            for quad in range(1 - o, 4):
+                row = 16 * o + 4 * quad
                 nc.sync.dma_start(
-                    planes[32 * quad : 32 * quad + 4, N * o : N * (o + 1)].bitcast(I32),
-                    scale_dealt[row : row + 4, :].bitcast(I32),
+                    planes[o][32 * quad : 32 * quad + 4, :].bitcast(I32), planes[0][row : row + 4, :].bitcast(I32)
                 )
 
         q_bf = keep.tile([P, PASSES, NQ, 4], BF16, name="q_bf", tag="words1", align_bytes=64)
@@ -111,7 +110,7 @@ def tile_attend_page_softcount_kernel(tc, qT, k_words, k_scales, rk, offs, out):
                 nc.tensor.transpose(turned[:, i, :], rk_dealt[:, HALF * h + P * i : HALF * h + P * (i + 1)], ident[:])
             nc.scalar.copy(rk6[:, 4 * h : 4 * h + 4], turned[:, :, P - 1])
 
-        keys = keep.tile([P, PASSES, 2 * N], U8, name="keys", align_bytes=64)
+        keys = {}
 
         gathered = keep.tile([P, N - RUN], U32, name="gathered", tag="words0", align_bytes=64)
 
@@ -123,8 +122,11 @@ def tile_attend_page_softcount_kernel(tc, qT, k_words, k_scales, rk, offs, out):
 
         def split(words, first, last):
             src = words.bitcast(U16).rearrange("p (j k s o) -> p o k j s", k=4, s=RUN, o=PASSES)
-            dst = keys[:].bitcast(U16).rearrange("p o (k j s) -> p o k j s", k=TILES, s=RUN)
-            nc.vector.tensor_copy(dst[:, :, first:last], src[:, :, first % 4 : (last - 1) % 4 + 1])
+            parted = keep.tile([P, PASSES, last - first, 2 * P], U8, name=f"keys{first}", align_bytes=64)
+            dst = parted[:].bitcast(U16).rearrange("p o k (j s) -> p o k j s", s=RUN)
+            nc.vector.tensor_copy(dst, src[:, :, first % 4 : (last - 1) % 4 + 1])
+            for k in range(first, last):
+                keys[k] = parted[:, :, k - first, :]
 
         match = keep.tile([P, N], F32, name="match")
         counts = keep.tile([P, N // SEG], F32, name="counts")
@@ -137,8 +139,8 @@ def tile_attend_page_softcount_kernel(tc, qT, k_words, k_scales, rk, offs, out):
             for o in range(PASSES):
                 nc.tensor.matmul_mx(
                     out=scores,
-                    lhsT=keys[:, o, 2 * P * k : 2 * P * (k + 1)].bitcast(FP4X4),
-                    lhsT_scale=planes[:, N * o + P * k : N * o + P * (k + 1)],
+                    lhsT=keys[k][:, o, :].bitcast(FP4X4),
+                    lhsT_scale=planes[o][:, P * k : P * (k + 1)],
                     rhs=q_codes[:, NQ * o : NQ * (o + 1)].bitcast(FP8X4),
                     rhs_scale=q_scales[:, NQ * o : NQ * (o + 1)],
                     start=(o == 0),

@@ -24,8 +24,7 @@ HALF = N // 2
 RUN = 8
 BANK = 512
 HEAD = 64
-FILLED = 2048
-ZERO_EARLY = 3072
+FILLED = 2560
 FLOPS = 2 * 1024 * N * NQ
 
 
@@ -40,7 +39,7 @@ def tile_attend_page_softcount_kernel(tc, qT, k_words, k_scales, rk, offs, out):
 
         offsets = keep.tile([P, N // 16], U16, name="offsets")
         scale_pool = keep.tile([P, T], U8, name="scale_pool")
-        rk_pool = keep.tile([P, T], F32, name="rk_pool", tag="lookup", align_bytes=64)
+        rk_pool = keep.tile([P, T], F32, name="rk_pool")
         word_pool = keep.tile([P, T], I32, name="word_pool")
         q_raw = keep.tile([P, PASSES, 4, NQ], F32, name="q_raw", tag="dealt0")
 
@@ -48,7 +47,7 @@ def tile_attend_page_softcount_kernel(tc, qT, k_words, k_scales, rk, offs, out):
         nc.sync.dma_start(
             scale_pool[0:32, :].bitcast(I32), k_scales.rearrange("o f t -> (o f) t").bitcast(I32)
         )
-        rk_head = keep.tile([P, HEAD], F32, name="rk_head")
+        rk_head = keep.tile([P, HEAD], F32, name="rk_head", tag="head", align_bytes=64)
         nc.sync.dma_start(rk_head[:], rk[:, 0:HEAD])
         nc.sync.dma_start(rk_pool[P - 1 : P, HEAD:T], rk[0:1, HEAD:T])
         nc.sync.dma_start(
@@ -56,7 +55,10 @@ def tile_attend_page_softcount_kernel(tc, qT, k_words, k_scales, rk, offs, out):
         )
         nc.sync.dma_start(word_pool[:], k_words[0].rearrange("p t b -> p (t b)").bitcast(I32))
 
-        planes = [keep.tile([P, N], U8, name=f"plane{o}", align_bytes=64) for o in range(PASSES)]
+        planes = [
+            keep.tile([P, N], U8, name="plane0", tag="head", align_bytes=64),
+            keep.tile([P, N], U8, name="plane1", align_bytes=64),
+        ]
         shift = keep.tile([P, 1], F32, name="shift")
         nc.vector.memset(shift[:], -6.0)
         nc.vector.memset(scale_pool[32:64, :].bitcast(I32), 0)
@@ -74,31 +76,34 @@ def tile_attend_page_softcount_kernel(tc, qT, k_words, k_scales, rk, offs, out):
             ACT.Copy,
         )
         scale_rows = keep.tile([P, N], U8, name="scale_rows")
-        nc.vector.memset(rk_pool[0 : P - 1, FILLED:ZERO_EARLY].bitcast(I32), 0)
+        nc.vector.memset(rk_pool[0 : P - 1, FILLED:T].bitcast(I32), 0)
         nc.vector.tensor_copy(scale_rows[:], scale_pool[:].indirect(offsets[:]))
-        nc.vector.memset(rk_pool[0 : P - 1, ZERO_EARLY:T].bitcast(I32), 0)
-        nc.vector.tensor_copy(
-            planes[0][:].bitcast(I32).rearrange("p (h k j w) -> p h k j w", h=2, k=4, w=2),
-            scale_rows[:].bitcast(I32).rearrange("p (h j k w) -> p h k j w", h=2, k=4, w=2),
-        )
 
-        for o in range(PASSES):
-            for quad in range(1 - o, 4):
-                row = 16 * o + 4 * quad
-                nc.sync.dma_start(
-                    planes[o][32 * quad : 32 * quad + 4, :].bitcast(I32), planes[0][row : row + 4, :].bitcast(I32)
-                )
-
-        q_bf = keep.tile([P, PASSES, NQ, 4], BF16, name="q_bf", tag="words1", align_bytes=64)
+        q_bf = keep.tile([P, PASSES, NQ, 4], BF16, name="q_bf", align_bytes=64)
         q_scales = keep.tile([P, PASSES * NQ], U8, name="q_scales", align_bytes=64)
         for o in range(PASSES):
             nc.scalar.copy(q_bf[:, o, :, :], q_raw[:, o, :, :].rearrange("p j w -> p w j"))
+
+        def place_scales():
+            nc.vector.tensor_copy(
+                planes[0][:].bitcast(I32).rearrange("p (h k j w) -> p h k j w", h=2, k=4, w=2),
+                scale_rows[:].bitcast(I32).rearrange("p (h j k w) -> p h k j w", h=2, k=4, w=2),
+            )
+
+            for o in range(PASSES):
+                for quad in range(1 - o, 4):
+                    row = 16 * o + 4 * quad
+                    nc.sync.dma_start(
+                        planes[o][32 * quad : 32 * quad + 4, :].bitcast(I32), planes[0][row : row + 4, :].bitcast(I32)
+                    )
 
         rk6 = keep.tile([P, TILES], F32, name="rk6")
         rk_dealt = keep.tile([P, N], F32, name="rk_dealt", tag="dealt0")
         for h in range(2):
             rk_slots = keep.tile([P, HALF], F32, name=f"rk_slots{h}", tag=f"words{2 * h}", align_bytes=64)
             nc.vector.tensor_copy(rk_slots[:], rk_pool[:].indirect(offsets[:, 32 * h : 32 * (h + 1)]))
+            if h == 0:
+                place_scales()
             nc.scalar.activation(
                 rk_dealt[:, HALF * h : HALF * (h + 1)].rearrange("p (k j s) -> p k j s", k=4, s=RUN),
                 rk_slots[:].rearrange("p (j k s) -> p k j s", k=4, s=RUN),
@@ -151,11 +156,11 @@ def tile_attend_page_softcount_kernel(tc, qT, k_words, k_scales, rk, offs, out):
             )
 
         def count(h):
+            terms = [match[:, P * k : P * (k + 1)] for k in range(4 * h, 4 * h + 4)]
             summed = in_bank(3 - 3 * h, f"summed{h}")[:, 0:P]
-            for i in range(4):
-                k = 4 * h + i
+            for i, term in enumerate(terms):
                 nc.tensor.matmul(
-                    summed, match[:, P * k : P * (k + 1)], ident[:], start=(i == 0), stop=(i == 3), is_transpose=True
+                    summed, term, ident[:], start=(i == 0), stop=(i == len(terms) - 1), is_transpose=True
                 )
             nc.vector.tensor_reduce(
                 counts[:, 16 * h : 16 * (h + 1)],
@@ -164,7 +169,7 @@ def tile_attend_page_softcount_kernel(tc, qT, k_words, k_scales, rk, offs, out):
                 mybir.AluOpType.add,
             )
 
-        q_codes = keep.tile([P, PASSES * NQ], U32, name="q_codes", tag="lookup", align_bytes=64)
+        q_codes = keep.tile([P, PASSES * NQ], U32, name="q_codes", align_bytes=64)
         for h in range(2):
             words = gather_words(h)
             if h == 0:

@@ -176,6 +176,15 @@ def tile_attend_page_softcount_kernel(tc, qT, k_words, k_scales, rk, offs, out):
                 nc.vector.quantize_mx(
                     out=q_codes[:].bitcast(FP8X4), scales=q_scales[:], in_=q_bf[:].rearrange("p o w j -> p (o w j)")
                 )
+                nc.tensor.matmul_mx(
+                    out=in_bank(3, "clock_warm")[:],
+                    lhsT=q_codes[:, 0:NQ].bitcast(FP8X4),
+                    lhsT_scale=q_scales[:, 0:NQ],
+                    rhs=gathered[:, HALF : HALF + BANK // 2].bitcast(FP4X4),
+                    rhs_scale=planes[0][:, 0:BANK],
+                    start=True,
+                    stop=True,
+                )
             split(words, 4 * h, 4 * h + 1)
             split(words, 4 * h + 1, 4 * h + 2)
             split(words, 4 * h + 2, 4 * h + 4)

@@ -24,7 +24,8 @@ HALF = N // 2
 RUN = 8
 BANK = 512
 HEAD = 64
-FILLED = 2560
+FILLED = 2048
+ZEROED_EARLY = 3072
 FLOPS = 2 * 1024 * N * NQ
 
 
@@ -41,22 +42,27 @@ def tile_attend_page_softcount_kernel(tc, qT, k_words, k_scales, rk, offs, out):
         scale_pool = keep.tile([P, T], U8, name="scale_pool")
         rk_pool = keep.tile([P, T], F32, name="rk_pool")
         word_pool = keep.tile([P, T], I32, name="word_pool")
-        q_raw = keep.tile([P, PASSES, 4, NQ], F32, name="q_raw", tag="dealt0")
+        rk_head = keep.tile([P, HEAD], F32, name="rk_head")
+        q_raw = [
+            keep.tile([P, 4, NQ], F32, name="q_raw0", tag="dealt"),
+            keep.tile([P, 4, NQ], F32, name="q_raw1", tag="columns"),
+        ]
+
+        def load_queries(o):
+            nc.sync.dma_start(q_raw[o][:], qT[0][BANK * o : BANK * (o + 1), :].rearrange("(p j) w -> p j w", j=4))
 
         nc.sync.dma_start(offsets[:], offs)
+        nc.sync.dma_start(rk_head[:], rk[:, 0:HEAD])
         nc.sync.dma_start(
             scale_pool[0:32, :].bitcast(I32), k_scales.rearrange("o f t -> (o f) t").bitcast(I32)
         )
-        rk_head = keep.tile([P, HEAD], F32, name="rk_head", tag="head", align_bytes=64)
-        nc.sync.dma_start(rk_head[:], rk[:, 0:HEAD])
         nc.sync.dma_start(rk_pool[P - 1 : P, HEAD:T], rk[0:1, HEAD:T])
-        nc.sync.dma_start(
-            q_raw[:].rearrange("p o j w -> p o (j w)"), qT[0].rearrange("(o p j) w -> p o (j w)", o=PASSES, j=4)
-        )
+        load_queries(0)
         nc.sync.dma_start(word_pool[:], k_words[0].rearrange("p t b -> p (t b)").bitcast(I32))
+        load_queries(1)
 
         planes = [
-            keep.tile([P, N], U8, name="plane0", tag="head", align_bytes=64),
+            keep.tile([P, N], U8, name="plane0", align_bytes=64),
             keep.tile([P, N], U8, name="plane1", align_bytes=64),
         ]
         shift = keep.tile([P, 1], F32, name="shift")
@@ -75,58 +81,64 @@ def tile_attend_page_softcount_kernel(tc, qT, k_words, k_scales, rk, offs, out):
             rk_head[0 : P - 1, :].unsqueeze(1).to_broadcast([P - 1, FILLED // HEAD - 1, HEAD]),
             ACT.Copy,
         )
-        scale_rows = keep.tile([P, N], U8, name="scale_rows")
-        nc.vector.memset(rk_pool[0 : P - 1, FILLED:T].bitcast(I32), 0)
+        scale_rows = keep.tile([P, N], U8, name="scale_rows", align_bytes=64)
+        nc.vector.memset(rk_pool[0 : P - 1, FILLED:ZEROED_EARLY].bitcast(I32), 0)
         nc.vector.tensor_copy(scale_rows[:], scale_pool[:].indirect(offsets[:]))
-
-        q_bf = keep.tile([P, PASSES, NQ, 4], BF16, name="q_bf", align_bytes=64)
-        q_scales = keep.tile([P, PASSES * NQ], U8, name="q_scales", align_bytes=64)
+        nc.vector.memset(rk_pool[0 : P - 1, ZEROED_EARLY:T].bitcast(I32), 0)
+        nc.vector.tensor_copy(
+            planes[0][:].bitcast(I32).rearrange("p (h k j w) -> p h k j w", h=2, k=4, w=2),
+            scale_rows[:].bitcast(I32).rearrange("p (h j k w) -> p h k j w", h=2, k=4, w=2),
+        )
         for o in range(PASSES):
-            nc.scalar.copy(q_bf[:, o, :, :], q_raw[:, o, :, :].rearrange("p j w -> p w j"))
+            for quad in range(1 - o, 4):
+                row = 16 * o + 4 * quad
+                nc.sync.dma_start(
+                    planes[o][32 * quad : 32 * quad + 4, :].bitcast(I32), planes[0][row : row + 4, :].bitcast(I32)
+                )
 
-        def place_scales():
-            nc.vector.tensor_copy(
-                planes[0][:].bitcast(I32).rearrange("p (h k j w) -> p h k j w", h=2, k=4, w=2),
-                scale_rows[:].bitcast(I32).rearrange("p (h j k w) -> p h k j w", h=2, k=4, w=2),
+        q_bf = {}
+        q_codes = [keep.tile([P, NQ], U32, name=f"q_codes{o}", align_bytes=64) for o in range(PASSES)]
+        q_scales = [keep.tile([P, NQ], U8, name=f"q_scales{o}", align_bytes=64) for o in range(PASSES)]
+
+        def cast(o, tag):
+            q_bf[o] = keep.tile([P, NQ, 4], BF16, name=f"q_bf{o}", tag=tag, align_bytes=64)
+            nc.scalar.copy(q_bf[o][:], q_raw[o][:].rearrange("p j w -> p w j"))
+
+        def quantize(o):
+            nc.vector.quantize_mx(
+                out=q_codes[o][:].bitcast(FP8X4), scales=q_scales[o][:], in_=q_bf[o][:].rearrange("p w j -> p (w j)")
             )
 
-            for o in range(PASSES):
-                for quad in range(1 - o, 4):
-                    row = 16 * o + 4 * quad
-                    nc.sync.dma_start(
-                        planes[o][32 * quad : 32 * quad + 4, :].bitcast(I32), planes[0][row : row + 4, :].bitcast(I32)
-                    )
-
-        rk6 = keep.tile([P, TILES], F32, name="rk6")
-        rk_dealt = keep.tile([P, N], F32, name="rk_dealt", tag="dealt0")
+        cast(0, "early")
+        turned = {}
+        rk_dealt = keep.tile([P, N], F32, name="rk_dealt", tag="dealt")
         for h in range(2):
-            rk_slots = keep.tile([P, HALF], F32, name=f"rk_slots{h}", tag=f"words{2 * h}", align_bytes=64)
+            rk_slots = keep.tile([P, HALF], F32, name=f"rk_slots{h}", tag=("words0", "late")[h], align_bytes=64)
             nc.vector.tensor_copy(rk_slots[:], rk_pool[:].indirect(offsets[:, 32 * h : 32 * (h + 1)]))
-            if h == 0:
-                place_scales()
             nc.scalar.activation(
                 rk_dealt[:, HALF * h : HALF * (h + 1)].rearrange("p (k j s) -> p k j s", k=4, s=RUN),
                 rk_slots[:].rearrange("p (j k s) -> p k j s", k=4, s=RUN),
                 ACT.Copy,
                 scale=6.0,
             )
-            turned = in_bank(3 + 4 * h, f"turned{h}")[:].rearrange("p (k m) -> p k m", m=P)
+            turned[h] = in_bank(3 + 4 * h, f"turned{h}")[:].rearrange("p (k m) -> p k m", m=P)
             for i in range(4):
-                nc.tensor.transpose(turned[:, i, :], rk_dealt[:, HALF * h + P * i : HALF * h + P * (i + 1)], ident[:])
-            nc.scalar.copy(rk6[:, 4 * h : 4 * h + 4], turned[:, :, P - 1])
+                nc.tensor.transpose(turned[h][:, i, :], rk_dealt[:, HALF * h + P * i : HALF * h + P * (i + 1)], ident[:])
+        quantize(0)
+        cast(1, "late")
+        rk6 = keep.tile([P, TILES], F32, name="rk6", tag="columns")
+        for h in range(2):
+            nc.scalar.copy(rk6[:, 4 * h : 4 * h + 4], turned[h][:, :, P - 1])
 
         keys = {}
 
-        gathered = keep.tile([P, N - RUN], U32, name="gathered", tag="words0", align_bytes=64)
-
-        def gather_words(h):
-            first = (1 - h) * (HALF - RUN)
-            words = gathered[:, first : first + HALF]
-            nc.vector.tensor_copy(words, word_pool[:].bitcast(U32).indirect(offsets[:, 32 * h : 32 * (h + 1)]))
+        def gather_words(h, tag):
+            words = keep.tile([P, HALF], U32, name=f"words{h}", tag=tag, align_bytes=64)
+            nc.vector.tensor_copy(words[:], word_pool[:].bitcast(U32).indirect(offsets[:, 32 * h : 32 * (h + 1)]))
             return words
 
         def split(words, first, last):
-            src = words.bitcast(U16).rearrange("p (j k s o) -> p o k j s", k=4, s=RUN, o=PASSES)
+            src = words[:].bitcast(U16).rearrange("p (j k s o) -> p o k j s", k=4, s=RUN, o=PASSES)
             parted = keep.tile([P, PASSES, last - first, 2 * P], U8, name=f"keys{first}", align_bytes=64)
             dst = parted[:].bitcast(U16).rearrange("p o k (j s) -> p o k j s", s=RUN)
             nc.vector.tensor_copy(dst, src[:, :, first % 4 : (last - 1) % 4 + 1])
@@ -135,24 +147,27 @@ def tile_attend_page_softcount_kernel(tc, qT, k_words, k_scales, rk, offs, out):
 
         match = keep.tile([P, N], F32, name="match")
         counts = keep.tile([P, N // SEG], F32, name="counts")
+        scores = {}
 
-        def score(k):
-            if k == 3:
-                scores = in_bank(4, "scores3", banks=4)[:, 0:NQ]
-            else:
-                scores = in_bank(k, f"scores{k}")[:, 0:NQ]
-            for o in range(PASSES):
-                nc.tensor.matmul_mx(
-                    out=scores,
-                    lhsT=keys[k][:, o, :].bitcast(FP4X4),
-                    lhsT_scale=planes[o][:, P * k : P * (k + 1)],
-                    rhs=q_codes[:, NQ * o : NQ * (o + 1)].bitcast(FP8X4),
-                    rhs_scale=q_scales[:, NQ * o : NQ * (o + 1)],
-                    start=(o == 0),
-                    stop=(o == PASSES - 1),
-                )
+        def product(k, o):
+            if o == 0:
+                if k == 3:
+                    scores[k] = in_bank(4, "scores3", banks=4)[:, 0:NQ]
+                else:
+                    scores[k] = in_bank(k, f"scores{k}")[:, 0:NQ]
+            nc.tensor.matmul_mx(
+                out=scores[k],
+                lhsT=keys[k][:, o, :].bitcast(FP4X4),
+                lhsT_scale=planes[o][:, P * k : P * (k + 1)],
+                rhs=q_codes[o][:].bitcast(FP8X4),
+                rhs_scale=q_scales[o][:],
+                start=(o == 0),
+                stop=(o == PASSES - 1),
+            )
+
+        def weigh(k):
             nc.scalar.activation(
-                match[:, P * k : P * (k + 1)], scores, ACT.Sigmoid, bias=shift[:], scale=rk6[:, k : k + 1]
+                match[:, P * k : P * (k + 1)], scores[k], ACT.Sigmoid, bias=shift[:], scale=rk6[:, k : k + 1]
             )
 
         def count(h):
@@ -169,27 +184,33 @@ def tile_attend_page_softcount_kernel(tc, qT, k_words, k_scales, rk, offs, out):
                 mybir.AluOpType.add,
             )
 
-        q_codes = keep.tile([P, PASSES * NQ], U32, name="q_codes", align_bytes=64)
-        for h in range(2):
-            words = gather_words(h)
-            if h == 0:
-                nc.vector.quantize_mx(
-                    out=q_codes[:].bitcast(FP8X4), scales=q_scales[:], in_=q_bf[:].rearrange("p o w j -> p (o w j)")
-                )
-                nc.tensor.matmul_mx(
-                    out=in_bank(3, "clock_warm")[:],
-                    lhsT=q_codes[:, 0:NQ].bitcast(FP8X4),
-                    lhsT_scale=q_scales[:, 0:NQ],
-                    rhs=gathered[:, HALF : HALF + BANK // 2].bitcast(FP4X4),
-                    rhs_scale=planes[0][:, 0:BANK],
-                    start=True,
-                    stop=True,
-                )
-            split(words, 4 * h, 4 * h + 1)
-            split(words, 4 * h + 1, 4 * h + 2)
-            split(words, 4 * h + 2, 4 * h + 4)
-        for h in range(2):
-            for k in range(4 * h, 4 * h + 4):
-                score(k)
-            count(h)
+        words = gather_words(0, "words0")
+        nc.tensor.matmul_mx(
+            out=in_bank(1, "clock_warm")[:],
+            lhsT=q_codes[0][:].bitcast(FP8X4),
+            lhsT_scale=q_scales[0][:],
+            rhs=words[:, 0 : BANK // 2].bitcast(FP4X4),
+            rhs_scale=scale_rows[:, 0:BANK],
+            start=True,
+            stop=True,
+        )
+        split(words, 0, 1)
+        split(words, 1, 2)
+        quantize(1)
+        split(words, 2, 4)
+        words = gather_words(1, "late")
+        split(words, 4, 5)
+        split(words, 5, 6)
+        split(words, 6, 8)
+        for o in range(PASSES):
+            for k in range(4):
+                product(k, o)
+        for k in range(4):
+            weigh(k)
+        count(0)
+        for k in range(4, 8):
+            for o in range(PASSES):
+                product(k, o)
+            weigh(k)
+        count(1)
         nc.sync.dma_start(out[0], counts[:])

@@ -24,8 +24,7 @@ HALF = N // 2
 RUN = 8
 BANK = 512
 HEAD = 64
-FILLED = 2048
-ZEROED_EARLY = 3072
+FILLED = 2688
 FLOPS = 2 * 1024 * N * NQ
 
 
@@ -82,9 +81,8 @@ def tile_attend_page_softcount_kernel(tc, qT, k_words, k_scales, rk, offs, out):
             ACT.Copy,
         )
         scale_rows = keep.tile([P, N], U8, name="scale_rows", align_bytes=64)
-        nc.vector.memset(rk_pool[0 : P - 1, FILLED:ZEROED_EARLY].bitcast(I32), 0)
+        nc.vector.memset(rk_pool[0 : P - 1, FILLED:T].bitcast(I32), 0)
         nc.vector.tensor_copy(scale_rows[:], scale_pool[:].indirect(offsets[:]))
-        nc.vector.memset(rk_pool[0 : P - 1, ZEROED_EARLY:T].bitcast(I32), 0)
         nc.vector.tensor_copy(
             planes[0][:].bitcast(I32).rearrange("p (h k j w) -> p h k j w", h=2, k=4, w=2),
             scale_rows[:].bitcast(I32).rearrange("p (h j k w) -> p h k j w", h=2, k=4, w=2),

@@ -25,6 +25,7 @@ RUN = 8
 BANK = 512
 HEAD = 64
 FILLED = 2688
+EARLY = 2
 FLOPS = 2 * 1024 * N * NQ
 
 
@@ -32,6 +33,7 @@ def tile_attend_page_softcount_kernel(tc, qT, k_words, k_scales, rk, offs, out):
     nc = tc.nc
     with ExitStack() as ctx:
         keep = ctx.enter_context(tc.tile_pool(name="keep", bufs=1))
+        shared = ctx.enter_context(tc.tile_pool(name="shared", bufs=1))
         psum = ctx.enter_context(tc.psum_pool(name="psum", bufs=1))
 
         def in_bank(bank, name, banks=1):
@@ -44,7 +46,7 @@ def tile_attend_page_softcount_kernel(tc, qT, k_words, k_scales, rk, offs, out):
         rk_head = keep.tile([P, HEAD], F32, name="rk_head")
         q_raw = [
             keep.tile([P, 4, NQ], F32, name="q_raw0", tag="dealt"),
-            keep.tile([P, 4, NQ], F32, name="q_raw1", tag="columns"),
+            shared.tile([P, 4, NQ], F32, name="q_raw1", offset=0),
         ]
 
         def load_queries(o):
@@ -119,62 +121,45 @@ def tile_attend_page_softcount_kernel(tc, qT, k_words, k_scales, rk, offs, out):
                 ACT.Copy,
                 scale=6.0,
             )
-            turned[h] = in_bank(3 + 4 * h, f"turned{h}")[:].rearrange("p (k m) -> p k m", m=P)
+            turned[h] = in_bank(6 + h, f"turned{h}")[:].rearrange("p (k m) -> p k m", m=P)
             for i in range(4):
                 nc.tensor.transpose(turned[h][:, i, :], rk_dealt[:, HALF * h + P * i : HALF * h + P * (i + 1)], ident[:])
         quantize(0)
         cast(1, "late")
-        rk6 = keep.tile([P, TILES], F32, name="rk6", tag="columns")
+        rk6 = shared.tile([P, TILES], F32, name="rk6", offset=0)
         for h in range(2):
             nc.scalar.copy(rk6[:, 4 * h : 4 * h + 4], turned[h][:, :, P - 1])
 
-        keys = {}
+        early_keys = keep.tile([P, EARLY, PASSES, 2 * P], U8, name="early_keys", align_bytes=64)
+        late_keys = shared.tile([P, TILES - EARLY, PASSES, 2 * P], U8, name="late_keys", offset=64, align_bytes=64)
+        keys = [early_keys[:, k] if k < EARLY else late_keys[:, k - EARLY] for k in range(TILES)]
+        words = [keep.tile([P, HALF], U32, name=f"words{h}", tag=f"words{h}", align_bytes=64) for h in range(2)]
 
-        def gather_words(h, tag):
-            words = keep.tile([P, HALF], U32, name=f"words{h}", tag=tag, align_bytes=64)
-            nc.vector.tensor_copy(words[:], word_pool[:].bitcast(U32).indirect(offsets[:, 32 * h : 32 * (h + 1)]))
-            return words
+        def gather_words(h):
+            nc.vector.tensor_copy(words[h][:], word_pool[:].bitcast(U32).indirect(offsets[:, 32 * h : 32 * (h + 1)]))
 
-        def split(words, first, last):
-            src = words[:].bitcast(U16).rearrange("p (j k s o) -> p o k j s", k=4, s=RUN, o=PASSES)
-            parted = keep.tile([P, PASSES, last - first, 2 * P], U8, name=f"keys{first}", align_bytes=64)
-            dst = parted[:].bitcast(U16).rearrange("p o k (j s) -> p o k j s", s=RUN)
-            nc.vector.tensor_copy(dst, src[:, :, first % 4 : (last - 1) % 4 + 1])
-            for k in range(first, last):
-                keys[k] = parted[:, :, k - first, :]
+        def split(k):
+            src = words[k // 4][:].bitcast(U16).rearrange("p (j k s o) -> p k o j s", k=4, s=RUN, o=PASSES)
+            nc.vector.tensor_copy(keys[k].bitcast(U16).rearrange("p o (j s) -> p o j s", s=RUN), src[:, k % 4])
 
-        match = keep.tile([P, N], F32, name="match")
+        match = [keep.tile([P, NQ], F32, name=f"match{k}") for k in range(TILES)]
         counts = keep.tile([P, N // SEG], F32, name="counts")
-        scores = {}
 
-        def product(k, o):
-            if o == 0:
-                if k == 3:
-                    scores[k] = in_bank(4, "scores3", banks=4)[:, 0:NQ]
-                else:
-                    scores[k] = in_bank(k, f"scores{k}")[:, 0:NQ]
+        def product(k, o, opens):
             nc.tensor.matmul_mx(
                 out=scores[k],
                 lhsT=keys[k][:, o, :].bitcast(FP4X4),
                 lhsT_scale=planes[o][:, P * k : P * (k + 1)],
                 rhs=q_codes[o][:].bitcast(FP8X4),
                 rhs_scale=q_scales[o][:],
-                start=(o == 0),
-                stop=(o == PASSES - 1),
+                start=opens,
+                stop=not opens,
             )
 
         def weigh(k):
-            nc.scalar.activation(
-                match[:, P * k : P * (k + 1)], scores[k], ACT.Sigmoid, bias=shift[:], scale=rk6[:, k : k + 1]
-            )
+            nc.scalar.activation(match[k][:], scores[k], ACT.Sigmoid, bias=shift[:], scale=rk6[:, k : k + 1])
 
-        def count(h):
-            terms = [match[:, P * k : P * (k + 1)] for k in range(4 * h, 4 * h + 4)]
-            summed = in_bank(3 - 3 * h, f"summed{h}")[:, 0:P]
-            for i, term in enumerate(terms):
-                nc.tensor.matmul(
-                    summed, term, ident[:], start=(i == 0), stop=(i == len(terms) - 1), is_transpose=True
-                )
+        def count(h, summed):
             nc.vector.tensor_reduce(
                 counts[:, 16 * h : 16 * (h + 1)],
                 summed.rearrange("p (j s) -> p j s", s=RUN),
@@ -182,33 +167,49 @@ def tile_attend_page_softcount_kernel(tc, qT, k_words, k_scales, rk, offs, out):
                 mybir.AluOpType.add,
             )
 
-        words = gather_words(0, "words0")
+        gather_words(0)
+        gather_words(1)
         nc.tensor.matmul_mx(
-            out=in_bank(1, "clock_warm")[:],
+            out=in_bank(5, "clock_warm")[:],
             lhsT=q_codes[0][:].bitcast(FP8X4),
             lhsT_scale=q_scales[0][:],
-            rhs=words[:, 0 : BANK // 2].bitcast(FP4X4),
+            rhs=words[0][:, 0 : BANK // 2].bitcast(FP4X4),
             rhs_scale=scale_rows[:, 0:BANK],
             start=True,
             stop=True,
         )
-        split(words, 0, 1)
-        split(words, 1, 2)
+        scores = [in_bank(k, f"scores{k}")[:, 0:NQ] for k in range(TILES)]
+        for k in range(EARLY):
+            split(k)
         quantize(1)
-        split(words, 2, 4)
-        words = gather_words(1, "late")
-        split(words, 4, 5)
-        split(words, 5, 6)
-        split(words, 6, 8)
+        for k in range(EARLY, TILES):
+            split(k)
         for o in range(PASSES):
-            for k in range(4):
-                product(k, o)
-        for k in range(4):
+            for k in range(EARLY):
+                product(k, o, o == 0)
+        for k in range(EARLY):
             weigh(k)
-        count(0)
-        for k in range(4, 8):
-            for o in range(PASSES):
-                product(k, o)
+        for k in range(EARLY, TILES):
+            product(k, 1, True)
+            product(k, 0, False)
             weigh(k)
-        count(1)
+
+        pairs = []
+        for k in (0, 2):
+            pair = keep.tile([P, NQ], F32, name=f"pair{k}")
+            nc.vector.tensor_add(pair[:], match[k][:], match[k + 1][:])
+            pairs.append(pair)
+        summed = [in_bank(6, "summed0")[:, 0:P], in_bank(5, "summed1")[:, 0:P]]
+
+        def turn(h, term, start, stop):
+            nc.tensor.matmul(summed[h], term[:], ident[:], start=start, stop=stop, is_transpose=True)
+
+        turn(1, match[4], True, False)
+        turn(1, match[5], False, False)
+        turn(0, pairs[0], True, False)
+        turn(0, pairs[1], False, True)
+        count(0, summed[0])
+        turn(1, match[6], False, False)
+        turn(1, match[7], False, True)
+        count(1, summed[1])
         nc.sync.dma_start(out[0], counts[:])

@@ -24,8 +24,9 @@ HALF = N // 2
 RUN = 8
 BANK = 512
 HEAD = 64
-FILLED = 2688
+FILLED = 1536
 EARLY = 2
+ZEROED = 2048
 FLOPS = 2 * 1024 * N * NQ
 
 
@@ -43,7 +44,7 @@ def tile_attend_page_softcount_kernel(tc, qT, k_words, k_scales, rk, offs, out):
         scale_pool = keep.tile([P, T], U8, name="scale_pool")
         rk_pool = keep.tile([P, T], F32, name="rk_pool")
         word_pool = keep.tile([P, T], I32, name="word_pool")
-        rk_head = keep.tile([P, HEAD], F32, name="rk_head")
+        rk_head = keep.tile([P, HEAD], F32, name="rk_head", tag="head", align_bytes=64)
         q_raw = [
             keep.tile([P, 4, NQ], F32, name="q_raw0", tag="dealt"),
             shared.tile([P, 4, NQ], F32, name="q_raw1", offset=0),
@@ -63,16 +64,23 @@ def tile_attend_page_softcount_kernel(tc, qT, k_words, k_scales, rk, offs, out):
         load_queries(1)
 
         planes = [
-            keep.tile([P, N], U8, name="plane0", align_bytes=64),
+            keep.tile([P, N], U8, name="plane0", tag="head", align_bytes=64),
             keep.tile([P, N], U8, name="plane1", align_bytes=64),
         ]
         shift = keep.tile([P, 1], F32, name="shift")
         nc.vector.memset(shift[:], -6.0)
-        nc.vector.memset(scale_pool[32:64, :].bitcast(I32), 0)
-        nc.vector.memset(scale_pool[64:128, :].bitcast(I32), 0)
-        nc.vector.memset(planes[1][:].bitcast(I32), 0)
+
+        def zero_beside_gpsimd(words):
+            cut = words.shape[1] // 2 + 1
+            nc.vector.memset(words[:, 0:cut], 0)
+            nc.vector.memset(words[:, cut:], 0)
+
+        zero_beside_gpsimd(scale_pool[32:64, :].bitcast(I32))
+        zero_beside_gpsimd(planes[1][:].bitcast(I32))
         ident = keep.tile([P, P], F32, name="ident")
         make_identity(nc, ident[:])
+        nc.gpsimd.memset(scale_pool[64:128, :].bitcast(I32), 0)
+        nc.gpsimd.memset(rk_pool[0 : P - 1, ZEROED:T].bitcast(I32), 0)
         table_warm = keep.tile([P, 1], F32, name="table_warm")
         nc.scalar.activation(table_warm[:], shift[:], ACT.Sigmoid)
 
@@ -83,18 +91,20 @@ def tile_attend_page_softcount_kernel(tc, qT, k_words, k_scales, rk, offs, out):
             ACT.Copy,
         )
         scale_rows = keep.tile([P, N], U8, name="scale_rows", align_bytes=64)
-        nc.vector.memset(rk_pool[0 : P - 1, FILLED:T].bitcast(I32), 0)
+        zero_beside_gpsimd(rk_pool[0 : P - 1, FILLED:ZEROED].bitcast(I32))
         nc.vector.tensor_copy(scale_rows[:], scale_pool[:].indirect(offsets[:]))
-        nc.vector.tensor_copy(
-            planes[0][:].bitcast(I32).rearrange("p (h k j w) -> p h k j w", h=2, k=4, w=2),
-            scale_rows[:].bitcast(I32).rearrange("p (h j k w) -> p h k j w", h=2, k=4, w=2),
-        )
-        for o in range(PASSES):
-            for quad in range(1 - o, 4):
-                row = 16 * o + 4 * quad
-                nc.sync.dma_start(
-                    planes[o][32 * quad : 32 * quad + 4, :].bitcast(I32), planes[0][row : row + 4, :].bitcast(I32)
-                )
+
+        def place_scales():
+            nc.vector.tensor_copy(
+                planes[0][:].bitcast(I32).rearrange("p (h k j w) -> p h k j w", h=2, k=4, w=2),
+                scale_rows[:].bitcast(I32).rearrange("p (h j k w) -> p h k j w", h=2, k=4, w=2),
+            )
+            for o in range(PASSES):
+                for quad in range(1 - o, 4):
+                    row = 16 * o + 4 * quad
+                    nc.sync.dma_start(
+                        planes[o][32 * quad : 32 * quad + 4, :].bitcast(I32), planes[0][row : row + 4, :].bitcast(I32)
+                    )
 
         q_bf = {}
         q_codes = [keep.tile([P, NQ], U32, name=f"q_codes{o}", align_bytes=64) for o in range(PASSES)]
@@ -115,6 +125,8 @@ def tile_attend_page_softcount_kernel(tc, qT, k_words, k_scales, rk, offs, out):
         for h in range(2):
             rk_slots = keep.tile([P, HALF], F32, name=f"rk_slots{h}", tag=("words0", "late")[h], align_bytes=64)
             nc.vector.tensor_copy(rk_slots[:], rk_pool[:].indirect(offsets[:, 32 * h : 32 * (h + 1)]))
+            if h == 0:
+                place_scales()
             nc.scalar.activation(
                 rk_dealt[:, HALF * h : HALF * (h + 1)].rearrange("p (k j s) -> p k j s", k=4, s=RUN),
                 rk_slots[:].rearrange("p (j k s) -> p k j s", k=4, s=RUN),

@@ -24,9 +24,9 @@ HALF = N // 2
 RUN = 8
 BANK = 512
 HEAD = 64
-FILLED = 1536
-EARLY = 2
-ZEROED = 2048
+FILLED = 2176
+EARLY = 1
+ZEROED = 800
 FLOPS = 2 * 1024 * N * NQ
 
 
@@ -44,7 +44,6 @@ def tile_attend_page_softcount_kernel(tc, qT, k_words, k_scales, rk, offs, out):
         scale_pool = keep.tile([P, T], U8, name="scale_pool")
         rk_pool = keep.tile([P, T], F32, name="rk_pool")
         word_pool = keep.tile([P, T], I32, name="word_pool")
-        rk_head = keep.tile([P, HEAD], F32, name="rk_head", tag="head", align_bytes=64)
         q_raw = [
             keep.tile([P, 4, NQ], F32, name="q_raw0", tag="dealt"),
             shared.tile([P, 4, NQ], F32, name="q_raw1", offset=0),
@@ -54,17 +53,16 @@ def tile_attend_page_softcount_kernel(tc, qT, k_words, k_scales, rk, offs, out):
             nc.sync.dma_start(q_raw[o][:], qT[0][BANK * o : BANK * (o + 1), :].rearrange("(p j) w -> p j w", j=4))
 
         nc.sync.dma_start(offsets[:], offs)
-        nc.sync.dma_start(rk_head[:], rk[:, 0:HEAD])
         nc.sync.dma_start(
             scale_pool[0:32, :].bitcast(I32), k_scales.rearrange("o f t -> (o f) t").bitcast(I32)
         )
-        nc.sync.dma_start(rk_pool[P - 1 : P, HEAD:T], rk[0:1, HEAD:T])
+        nc.sync.dma_start(rk_pool[P - 1 : P, :], rk[0:1, :])
         load_queries(0)
         nc.sync.dma_start(word_pool[:], k_words[0].rearrange("p t b -> p (t b)").bitcast(I32))
         load_queries(1)
 
         planes = [
-            keep.tile([P, N], U8, name="plane0", tag="head", align_bytes=64),
+            keep.tile([P, N], U8, name="plane0", align_bytes=64),
             keep.tile([P, N], U8, name="plane1", align_bytes=64),
         ]
         shift = keep.tile([P, 1], F32, name="shift")
@@ -76,22 +74,16 @@ def tile_attend_page_softcount_kernel(tc, qT, k_words, k_scales, rk, offs, out):
             nc.vector.memset(words[:, cut:], 0)
 
         zero_beside_gpsimd(scale_pool[32:64, :].bitcast(I32))
-        zero_beside_gpsimd(planes[1][:].bitcast(I32))
-        ident = keep.tile([P, P], F32, name="ident")
-        make_identity(nc, ident[:])
         nc.gpsimd.memset(scale_pool[64:128, :].bitcast(I32), 0)
         nc.gpsimd.memset(rk_pool[0 : P - 1, ZEROED:T].bitcast(I32), 0)
+        nc.gpsimd.memset(planes[1][:].bitcast(I32), 0)
+        ident = keep.tile([P, P], F32, name="ident")
+        make_identity(nc, ident[:])
         table_warm = keep.tile([P, 1], F32, name="table_warm")
         nc.scalar.activation(table_warm[:], shift[:], ACT.Sigmoid)
 
-        nc.scalar.activation(rk_pool[:, 0:HEAD], rk_head[:], ACT.Copy)
-        nc.scalar.activation(
-            rk_pool[0 : P - 1, HEAD:FILLED].rearrange("p (r c) -> p r c", c=HEAD),
-            rk_head[0 : P - 1, :].unsqueeze(1).to_broadcast([P - 1, FILLED // HEAD - 1, HEAD]),
-            ACT.Copy,
-        )
         scale_rows = keep.tile([P, N], U8, name="scale_rows", align_bytes=64)
-        zero_beside_gpsimd(rk_pool[0 : P - 1, FILLED:ZEROED].bitcast(I32))
+        zero_beside_gpsimd(rk_pool[0 : P - 1, 0:ZEROED].bitcast(I32))
         nc.vector.tensor_copy(scale_rows[:], scale_pool[:].indirect(offsets[:]))
 
         def place_scales():

@@ -23,8 +23,6 @@ TILES = N // P
 HALF = N // 2
 RUN = 8
 BANK = 512
-HEAD = 64
-FILLED = 2176
 EARLY = 1
 ZEROED = 800
 FLOPS = 2 * 1024 * N * NQ
@@ -52,10 +50,10 @@ def tile_attend_page_softcount_kernel(tc, qT, k_words, k_scales, rk, offs, out):
         def load_queries(o):
             nc.sync.dma_start(q_raw[o][:], qT[0][BANK * o : BANK * (o + 1), :].rearrange("(p j) w -> p j w", j=4))
 
-        nc.sync.dma_start(offsets[:], offs)
         nc.sync.dma_start(
             scale_pool[0:32, :].bitcast(I32), k_scales.rearrange("o f t -> (o f) t").bitcast(I32)
         )
+        nc.sync.dma_start(offsets[:], offs)
         nc.sync.dma_start(rk_pool[P - 1 : P, :], rk[0:1, :])
         load_queries(0)
         nc.sync.dma_start(word_pool[:], k_words[0].rearrange("p t b -> p (t b)").bitcast(I32))
@@ -104,7 +102,9 @@ def tile_attend_page_softcount_kernel(tc, qT, k_words, k_scales, rk, offs, out):
 
         def cast(o, tag):
             q_bf[o] = keep.tile([P, NQ, 4], BF16, name=f"q_bf{o}", tag=tag, align_bytes=64)
-            nc.scalar.copy(q_bf[o][:], q_raw[o][:].rearrange("p j w -> p w j"))
+            nc.scalar.copy(
+                q_bf[o][:].rearrange("p (c i) j -> p c j i", i=4), q_raw[o][:].rearrange("p j (c i) -> p c j i", i=4)
+            )
 
         def quantize(o):
             nc.vector.quantize_mx(
@@ -203,16 +203,16 @@ def tile_attend_page_softcount_kernel(tc, qT, k_words, k_scales, rk, offs, out):
             pair = keep.tile([P, NQ], F32, name=f"pair{k}")
             nc.vector.tensor_add(pair[:], match[k][:], match[k + 1][:])
             pairs.append(pair)
-        summed = [in_bank(6, "summed0")[:, 0:P], in_bank(5, "summed1")[:, 0:P]]
+        summed = [in_bank(4, "summed0")[:, 0:P], in_bank(3, "summed1")[:, 0:P]]
 
         def turn(h, term, start, stop):
             nc.tensor.matmul(summed[h], term[:], ident[:], start=start, stop=stop, is_transpose=True)
 
-        turn(1, match[4], True, False)
-        turn(1, match[5], False, False)
         turn(0, pairs[0], True, False)
         turn(0, pairs[1], False, True)
         count(0, summed[0])
+        turn(1, match[4], True, False)
+        turn(1, match[5], False, False)
         turn(1, match[6], False, False)
         turn(1, match[7], False, True)
         count(1, summed[1])

@@ -24,7 +24,8 @@ HALF = N // 2
 RUN = 8
 BANK = 512
 EARLY = 1
-ZEROED = 800
+ZEROED_EARLY = 640
+ZEROED = 1120
 FLOPS = 2 * 1024 * N * NQ
 
 
@@ -81,8 +82,9 @@ def tile_attend_page_softcount_kernel(tc, qT, k_words, k_scales, rk, offs, out):
         nc.scalar.activation(table_warm[:], shift[:], ACT.Sigmoid)
 
         scale_rows = keep.tile([P, N], U8, name="scale_rows", align_bytes=64)
-        zero_beside_gpsimd(rk_pool[0 : P - 1, 0:ZEROED].bitcast(I32))
+        zero_beside_gpsimd(rk_pool[0 : P - 1, 0:ZEROED_EARLY].bitcast(I32))
         nc.vector.tensor_copy(scale_rows[:], scale_pool[:].indirect(offsets[:]))
+        zero_beside_gpsimd(rk_pool[0 : P - 1, ZEROED_EARLY:ZEROED].bitcast(I32))
 
         def place_scales():
             nc.vector.tensor_copy(
@@ -96,6 +98,7 @@ def tile_attend_page_softcount_kernel(tc, qT, k_words, k_scales, rk, offs, out):
                         planes[o][32 * quad : 32 * quad + 4, :].bitcast(I32), planes[0][row : row + 4, :].bitcast(I32)
                     )
 
+        place_scales()
         q_bf = {}
         q_codes = [keep.tile([P, NQ], U32, name=f"q_codes{o}", align_bytes=64) for o in range(PASSES)]
         q_scales = [keep.tile([P, NQ], U8, name=f"q_scales{o}", align_bytes=64) for o in range(PASSES)]
@@ -117,16 +120,14 @@ def tile_attend_page_softcount_kernel(tc, qT, k_words, k_scales, rk, offs, out):
         for h in range(2):
             rk_slots = keep.tile([P, HALF], F32, name=f"rk_slots{h}", tag=("words0", "late")[h], align_bytes=64)
             nc.vector.tensor_copy(rk_slots[:], rk_pool[:].indirect(offsets[:, 32 * h : 32 * (h + 1)]))
-            if h == 0:
-                place_scales()
-            nc.scalar.activation(
-                rk_dealt[:, HALF * h : HALF * (h + 1)].rearrange("p (k j s) -> p k j s", k=4, s=RUN),
-                rk_slots[:].rearrange("p (j k s) -> p k j s", k=4, s=RUN),
-                ACT.Copy,
-                scale=6.0,
-            )
             turned[h] = in_bank(6 + h, f"turned{h}")[:].rearrange("p (k m) -> p k m", m=P)
             for i in range(4):
+                nc.scalar.activation(
+                    rk_dealt[:, HALF * h + P * i : HALF * h + P * (i + 1)].rearrange("p (j s) -> p j s", s=RUN),
+                    rk_slots[:].rearrange("p (j k s) -> p k j s", k=4, s=RUN)[:, i],
+                    ACT.Copy,
+                    scale=6.0,
+                )
                 nc.tensor.transpose(turned[h][:, i, :], rk_dealt[:, HALF * h + P * i : HALF * h + P * (i + 1)], ident[:])
         quantize(0)
         cast(1, "late")

@@ -174,15 +174,6 @@ def tile_attend_page_softcount_kernel(tc, qT, k_words, k_scales, rk, offs, out):
 
         gather_words(0)
         gather_words(1)
-        nc.tensor.matmul_mx(
-            out=in_bank(5, "clock_warm")[:],
-            lhsT=q_codes[0][:].bitcast(FP8X4),
-            lhsT_scale=q_scales[0][:],
-            rhs=words[0][:, 0 : BANK // 2].bitcast(FP4X4),
-            rhs_scale=scale_rows[:, 0:BANK],
-            start=True,
-            stop=True,
-        )
         scores = [in_bank(k, f"scores{k}")[:, 0:NQ] for k in range(TILES)]
         for k in range(EARLY):
             split(k)

@@ -23,7 +23,6 @@ TILES = N // P
 HALF = N // 2
 RUN = 8
 BANK = 512
-EARLY = 1
 ZEROED_EARLY = 640
 ZEROED = 1120
 FLOPS = 2 * 1024 * N * NQ
@@ -135,17 +134,32 @@ def tile_attend_page_softcount_kernel(tc, qT, k_words, k_scales, rk, offs, out):
         for h in range(2):
             nc.scalar.copy(rk6[:, 4 * h : 4 * h + 4], turned[h][:, :, P - 1])
 
-        early_keys = keep.tile([P, EARLY, PASSES, 2 * P], U8, name="early_keys", align_bytes=64)
-        late_keys = shared.tile([P, TILES - EARLY, PASSES, 2 * P], U8, name="late_keys", offset=64, align_bytes=64)
-        keys = [early_keys[:, k] if k < EARLY else late_keys[:, k - EARLY] for k in range(TILES)]
+        first_keys = [
+            keep.tile([P, 4, 2 * P], U8, name="first_keys0", align_bytes=64),
+            shared.tile([P, 4, 2 * P], U8, name="first_keys1", offset=64, align_bytes=64),
+        ]
+        late_keys = shared.tile([P, 4, PASSES, 2 * P], U8, name="late_keys", offset=64 + 8 * P, align_bytes=64)
         words = [keep.tile([P, HALF], U32, name=f"words{h}", tag=f"words{h}", align_bytes=64) for h in range(2)]
+
+        def keys(k, o):
+            return first_keys[o][:, k, :] if k < 4 else late_keys[:, k - 4, o, :]
 
         def gather_words(h):
             nc.vector.tensor_copy(words[h][:], word_pool[:].bitcast(U32).indirect(offsets[:, 32 * h : 32 * (h + 1)]))
 
+        def halves(h):
+            return words[h][:].bitcast(U16).rearrange("p (j k s o) -> p k o j s", k=4, s=RUN, o=PASSES)
+
+        def split_pair(k, o):
+            nc.vector.tensor_copy(
+                first_keys[o][:, k : k + 2, :].bitcast(U16).rearrange("p k (j s) -> p k j s", s=RUN),
+                halves(0)[:, k : k + 2, o],
+            )
+
         def split(k):
-            src = words[k // 4][:].bitcast(U16).rearrange("p (j k s o) -> p k o j s", k=4, s=RUN, o=PASSES)
-            nc.vector.tensor_copy(keys[k].bitcast(U16).rearrange("p o (j s) -> p o j s", s=RUN), src[:, k % 4])
+            nc.vector.tensor_copy(
+                late_keys[:, k - 4].bitcast(U16).rearrange("p o (j s) -> p o j s", s=RUN), halves(1)[:, k - 4]
+            )
 
         match = [keep.tile([P, NQ], F32, name=f"match{k}") for k in range(TILES)]
         counts = keep.tile([P, N // SEG], F32, name="counts")
@@ -153,7 +167,7 @@ def tile_attend_page_softcount_kernel(tc, qT, k_words, k_scales, rk, offs, out):
         def product(k, o, opens):
             nc.tensor.matmul_mx(
                 out=scores[k],
-                lhsT=keys[k][:, o, :].bitcast(FP4X4),
+                lhsT=keys(k, o).bitcast(FP4X4),
                 lhsT_scale=planes[o][:, P * k : P * (k + 1)],
                 rhs=q_codes[o][:].bitcast(FP8X4),
                 rhs_scale=q_scales[o][:],
@@ -175,17 +189,19 @@ def tile_attend_page_softcount_kernel(tc, qT, k_words, k_scales, rk, offs, out):
         gather_words(0)
         gather_words(1)
         scores = [in_bank(k, f"scores{k}")[:, 0:NQ] for k in range(TILES)]
-        for k in range(EARLY):
-            split(k)
+        for k in (0, 2):
+            split_pair(k, 0)
         quantize(1)
-        for k in range(EARLY, TILES):
+        for k in (0, 2):
+            split_pair(k, 1)
+        for k in range(4, TILES):
             split(k)
-        for o in range(PASSES):
-            for k in range(EARLY):
-                product(k, o, o == 0)
-        for k in range(EARLY):
+        for k in range(4):
+            product(k, 0, True)
+        for k in range(4):
+            product(k, 1, False)
             weigh(k)
-        for k in range(EARLY, TILES):
+        for k in range(4, TILES):
             product(k, 1, True)
             product(k, 0, False)
             weigh(k)

@@ -21,7 +21,8 @@ PASSES = 2
 SEG = 32
 TILES = N // P
 HALF = N // 2
-RUN = 8
+QUARTER = N // 4
+RUNS = (8, 16)
 BANK = 512
 ZEROED_EARLY = 640
 ZEROED = 1120
@@ -87,8 +88,12 @@ def tile_attend_page_softcount_kernel(tc, qT, k_words, k_scales, rk, offs, out):
 
         def place_scales():
             nc.vector.tensor_copy(
-                planes[0][:].bitcast(I32).rearrange("p (h k j w) -> p h k j w", h=2, k=4, w=2),
-                scale_rows[:].bitcast(I32).rearrange("p (h j k w) -> p h k j w", h=2, k=4, w=2),
+                planes[0][:, 0:HALF].bitcast(I32).rearrange("p (k j w) -> p k j w", k=4, w=2),
+                scale_rows[:, 0:HALF].bitcast(I32).rearrange("p (j k w) -> p k j w", k=4, w=2),
+            )
+            nc.vector.tensor_copy(
+                planes[0][:, HALF:N].bitcast(I32).rearrange("p (c k j w) -> p c k j w", c=2, k=2, w=4),
+                scale_rows[:, HALF:N].bitcast(I32).rearrange("p (c j k w) -> p c k j w", c=2, k=2, w=4),
             )
             for o in range(PASSES):
                 for quad in range(1 - o, 4):
@@ -117,13 +122,15 @@ def tile_attend_page_softcount_kernel(tc, qT, k_words, k_scales, rk, offs, out):
         turned = {}
         rk_dealt = keep.tile([P, N], F32, name="rk_dealt", tag="dealt")
         for h in range(2):
-            rk_slots = keep.tile([P, HALF], F32, name=f"rk_slots{h}", tag=("words0", "late")[h], align_bytes=64)
+            rk_slots = keep.tile([P, HALF], F32, name=f"rk_slots{h}", tag=("words0", "late")[h], align_bytes=(32, 64)[h])
             nc.vector.tensor_copy(rk_slots[:], rk_pool[:].indirect(offsets[:, 32 * h : 32 * (h + 1)]))
             turned[h] = in_bank(6 + h, f"turned{h}")[:].rearrange("p (k m) -> p k m", m=P)
+            groups = h + 1
+            by_tile = rk_slots[:].rearrange("p (c j k s) -> p c k j s", c=groups, k=4 // groups, s=RUNS[h])
             for i in range(4):
                 nc.scalar.activation(
-                    rk_dealt[:, HALF * h + P * i : HALF * h + P * (i + 1)].rearrange("p (j s) -> p j s", s=RUN),
-                    rk_slots[:].rearrange("p (j k s) -> p k j s", k=4, s=RUN)[:, i],
+                    rk_dealt[:, HALF * h + P * i : HALF * h + P * (i + 1)].rearrange("p (j s) -> p j s", s=RUNS[h]),
+                    by_tile[:, i * groups // 4, i % (4 // groups)],
                     ACT.Copy,
                     scale=6.0,
                 )
@@ -135,30 +142,38 @@ def tile_attend_page_softcount_kernel(tc, qT, k_words, k_scales, rk, offs, out):
             nc.scalar.copy(rk6[:, 4 * h : 4 * h + 4], turned[h][:, :, P - 1])
 
         first_keys = [
-            keep.tile([P, 4, 2 * P], U8, name="first_keys0", align_bytes=64),
-            shared.tile([P, 4, 2 * P], U8, name="first_keys1", offset=64, align_bytes=64),
+            keep.tile([P, 6, 2 * P], U8, name="first_keys0", align_bytes=64),
+            shared.tile([P, 6, 2 * P], U8, name="first_keys1", offset=64, align_bytes=64),
         ]
-        late_keys = shared.tile([P, 4, PASSES, 2 * P], U8, name="late_keys", offset=64 + 8 * P, align_bytes=64)
-        words = [keep.tile([P, HALF], U32, name=f"words{h}", tag=f"words{h}", align_bytes=64) for h in range(2)]
+        late_keys = keep.tile([P, 2, PASSES, 2 * P], U8, name="late_keys", align_bytes=64)
+        words = [
+            keep.tile([P, HALF], U32, name="words0", tag="words0", align_bytes=32),
+            keep.tile([P, QUARTER], U32, name="words1"),
+            shared.tile([P, QUARTER], U32, name="words2", offset=64 + 12 * P),
+        ]
+        starts = (0, HALF, HALF + QUARTER, N)
 
         def keys(k, o):
-            return first_keys[o][:, k, :] if k < 4 else late_keys[:, k - 4, o, :]
+            return first_keys[o][:, k, :] if k < 6 else late_keys[:, k - 6, o, :]
 
-        def gather_words(h):
-            nc.vector.tensor_copy(words[h][:], word_pool[:].bitcast(U32).indirect(offsets[:, 32 * h : 32 * (h + 1)]))
+        def gather_words(g):
+            listed = offsets[:, starts[g] // 16 : starts[g + 1] // 16]
+            nc.vector.tensor_copy(words[g][:], word_pool[:].bitcast(U32).indirect(listed))
 
-        def halves(h):
-            return words[h][:].bitcast(U16).rearrange("p (j k s o) -> p k o j s", k=4, s=RUN, o=PASSES)
+        def halves(g):
+            run = RUNS[min(g, 1)]
+            return words[g][:].bitcast(U16).rearrange("p (j k s o) -> p k o j s", k=32 // run, s=run, o=PASSES)
 
         def split_pair(k, o):
+            g = k // 4
             nc.vector.tensor_copy(
-                first_keys[o][:, k : k + 2, :].bitcast(U16).rearrange("p k (j s) -> p k j s", s=RUN),
-                halves(0)[:, k : k + 2, o],
+                first_keys[o][:, k : k + 2, :].bitcast(U16).rearrange("p k (j s) -> p k j s", s=RUNS[g]),
+                halves(g)[:, k % 4 : k % 4 + 2, o],
             )
 
         def split(k):
             nc.vector.tensor_copy(
-                late_keys[:, k - 4].bitcast(U16).rearrange("p o (j s) -> p o j s", s=RUN), halves(1)[:, k - 4]
+                late_keys[:, k - 6].bitcast(U16).rearrange("p o (j s) -> p o j s", s=RUNS[1]), halves(2)[:, k - 6]
             )
 
         match = [keep.tile([P, NQ], F32, name=f"match{k}") for k in range(TILES)]
@@ -178,10 +193,10 @@ def tile_attend_page_softcount_kernel(tc, qT, k_words, k_scales, rk, offs, out):
         def weigh(k):
             nc.scalar.activation(match[k][:], scores[k], ACT.Sigmoid, bias=shift[:], scale=rk6[:, k : k + 1])
 
-        def count(h, summed):
+        def count(first, run, summed):
             nc.vector.tensor_reduce(
-                counts[:, 16 * h : 16 * (h + 1)],
-                summed.rearrange("p (j s) -> p j s", s=RUN),
+                counts[:, first : first + P // run],
+                summed.rearrange("p (j s) -> p j s", s=run),
                 mybir.AxisListType.X,
                 mybir.AluOpType.add,
             )
@@ -189,19 +204,21 @@ def tile_attend_page_softcount_kernel(tc, qT, k_words, k_scales, rk, offs, out):
         gather_words(0)
         gather_words(1)
         scores = [in_bank(k, f"scores{k}")[:, 0:NQ] for k in range(TILES)]
-        for k in (0, 2):
+        for k in (0, 2, 4):
             split_pair(k, 0)
         quantize(1)
         for k in (0, 2):
             split_pair(k, 1)
-        for k in range(4, TILES):
+        gather_words(2)
+        split_pair(4, 1)
+        for k in (6, 7):
             split(k)
-        for k in range(4):
+        for k in range(6):
             product(k, 0, True)
-        for k in range(4):
+        for k in range(6):
             product(k, 1, False)
             weigh(k)
-        for k in range(4, TILES):
+        for k in (6, 7):
             product(k, 1, True)
             product(k, 0, False)
             weigh(k)
@@ -211,17 +228,14 @@ def tile_attend_page_softcount_kernel(tc, qT, k_words, k_scales, rk, offs, out):
             pair = keep.tile([P, NQ], F32, name=f"pair{k}")
             nc.vector.tensor_add(pair[:], match[k][:], match[k + 1][:])
             pairs.append(pair)
-        summed = [in_bank(4, "summed0")[:, 0:P], in_bank(3, "summed1")[:, 0:P]]
 
-        def turn(h, term, start, stop):
-            nc.tensor.matmul(summed[h], term[:], ident[:], start=start, stop=stop, is_transpose=True)
+        def turn_and_count(bank, terms, first, run):
+            summed = in_bank(bank, f"summed{bank}")[:, 0:P]
+            for i, term in enumerate(terms):
+                nc.tensor.matmul(summed, term[:], ident[:], start=i == 0, stop=i == 1, is_transpose=True)
+            count(first, run, summed)
 
-        turn(0, pairs[0], True, False)
-        turn(0, pairs[1], False, True)
-        count(0, summed[0])
-        turn(1, match[4], True, False)
-        turn(1, match[5], False, False)
-        turn(1, match[6], False, False)
-        turn(1, match[7], False, True)
-        count(1, summed[1])
+        turn_and_count(4, pairs, 0, RUNS[0])
+        turn_and_count(3, match[4:6], 16, RUNS[1])
+        turn_and_count(2, match[6:8], 24, RUNS[1])
         nc.sync.dma_start(out[0], counts[:])

@@ -75,31 +75,33 @@ def tile_attend_page_softcount_kernel(tc, qT, k_words, k_scales, rk, offs, out):
         zero_beside_gpsimd(scale_pool[32:64, :].bitcast(I32))
         nc.gpsimd.memset(scale_pool[64:128, :].bitcast(I32), 0)
         nc.gpsimd.memset(rk_pool[0 : P - 1, ZEROED:T].bitcast(I32), 0)
-        nc.gpsimd.memset(planes[1][:].bitcast(I32), 0)
+        for o in range(PASSES):
+            nc.gpsimd.memset(planes[o][:].bitcast(I32), 0)
         ident = keep.tile([P, P], F32, name="ident")
         make_identity(nc, ident[:])
         table_warm = keep.tile([P, 1], F32, name="table_warm")
         nc.scalar.activation(table_warm[:], shift[:], ACT.Sigmoid)
 
         scale_rows = keep.tile([P, N], U8, name="scale_rows", align_bytes=64)
+        scale_dealt = keep.tile([P, N], U8, name="scale_dealt", align_bytes=64)
         zero_beside_gpsimd(rk_pool[0 : P - 1, 0:ZEROED_EARLY].bitcast(I32))
         nc.vector.tensor_copy(scale_rows[:], scale_pool[:].indirect(offsets[:]))
         zero_beside_gpsimd(rk_pool[0 : P - 1, ZEROED_EARLY:ZEROED].bitcast(I32))
 
         def place_scales():
             nc.vector.tensor_copy(
-                planes[0][:, 0:HALF].bitcast(I32).rearrange("p (k j w) -> p k j w", k=4, w=2),
+                scale_dealt[:, 0:HALF].bitcast(I32).rearrange("p (k j w) -> p k j w", k=4, w=2),
                 scale_rows[:, 0:HALF].bitcast(I32).rearrange("p (j k w) -> p k j w", k=4, w=2),
             )
             nc.vector.tensor_copy(
-                planes[0][:, HALF:N].bitcast(I32).rearrange("p (c k j w) -> p c k j w", c=2, k=2, w=4),
+                scale_dealt[:, HALF:N].bitcast(I32).rearrange("p (c k j w) -> p c k j w", c=2, k=2, w=4),
                 scale_rows[:, HALF:N].bitcast(I32).rearrange("p (c j k w) -> p c k j w", c=2, k=2, w=4),
             )
             for o in range(PASSES):
-                for quad in range(1 - o, 4):
-                    row = 16 * o + 4 * quad
+                for j in range(4):
+                    row = 16 * o + j
                     nc.sync.dma_start(
-                        planes[o][32 * quad : 32 * quad + 4, :].bitcast(I32), planes[0][row : row + 4, :].bitcast(I32)
+                        planes[o][j:P:32, :].bitcast(I32), scale_dealt[row : row + 13 : 4, :].bitcast(I32)
                     )
 
         place_scales()

from contextlib import ExitStack

import concourse.mybir as mybir
from concourse.masks import make_identity

F32 = mybir.dt.float32
BF16 = mybir.dt.bfloat16
I32 = mybir.dt.int32
U32 = mybir.dt.uint32
U16 = mybir.dt.uint16
U8 = mybir.dt.uint8
FP8X4 = mybir.dt.float8_e4m3fn_x4
FP4X4 = mybir.dt.float4_e2m1fn_x4
ACT = mybir.ActivationFunctionType

P = 128
T = 4096
N = 1024
NQ = 128
PASSES = 2
SEG = 32
TILES = N // P
HALF = N // 2
QUARTER = N // 4
RUNS = (8, 16)
BANK = 512
ZEROED_EARLY = 640
ZEROED = 1120
FLOPS = 2 * 1024 * N * NQ


def tile_attend_page_softcount_kernel(tc, qT, k_words, k_scales, rk, offs, out):
    nc = tc.nc
    with ExitStack() as ctx:
        keep = ctx.enter_context(tc.tile_pool(name="keep", bufs=1))
        shared = ctx.enter_context(tc.tile_pool(name="shared", bufs=1))
        psum = ctx.enter_context(tc.psum_pool(name="psum", bufs=1))

        def in_bank(bank, name, banks=1):
            return psum.tile([P, banks * BANK], F32, name=name, offset=4 * BANK * bank)

        offsets = keep.tile([P, N // 16], U16, name="offsets")
        scale_pool = keep.tile([P, T], U8, name="scale_pool")
        rk_pool = keep.tile([P, T], F32, name="rk_pool")
        word_pool = keep.tile([P, T], I32, name="word_pool")
        q_raw = [
            keep.tile([P, 4, NQ], F32, name="q_raw0", tag="dealt"),
            shared.tile([P, 4, NQ], F32, name="q_raw1", offset=0),
        ]

        def load_queries(o):
            nc.sync.dma_start(q_raw[o][:], qT[0][BANK * o : BANK * (o + 1), :].rearrange("(p j) w -> p j w", j=4))

        nc.sync.dma_start(
            scale_pool[0:32, :].bitcast(I32), k_scales.rearrange("o f t -> (o f) t").bitcast(I32)
        )
        nc.sync.dma_start(offsets[:], offs)
        nc.sync.dma_start(rk_pool[P - 1 : P, :], rk[0:1, :])
        load_queries(0)
        nc.sync.dma_start(word_pool[:], k_words[0].rearrange("p t b -> p (t b)").bitcast(I32))
        load_queries(1)

        planes = [
            keep.tile([P, N], U8, name="plane0", align_bytes=64),
            keep.tile([P, N], U8, name="plane1", align_bytes=64),
        ]
        shift = keep.tile([P, 1], F32, name="shift")
        nc.vector.memset(shift[:], -6.0)

        def zero_beside_gpsimd(words):
            cut = words.shape[1] // 2 + 1
            nc.vector.memset(words[:, 0:cut], 0)
            nc.vector.memset(words[:, cut:], 0)

        zero_beside_gpsimd(scale_pool[32:64, :].bitcast(I32))
        nc.gpsimd.memset(scale_pool[64:128, :].bitcast(I32), 0)
        nc.gpsimd.memset(rk_pool[0 : P - 1, ZEROED:T].bitcast(I32), 0)
        for o in range(PASSES):
            nc.gpsimd.memset(planes[o][:].bitcast(I32), 0)
        ident = keep.tile([P, P], F32, name="ident")
        make_identity(nc, ident[:])
        table_warm = keep.tile([P, 1], F32, name="table_warm")
        nc.scalar.activation(table_warm[:], shift[:], ACT.Sigmoid)

        scale_rows = keep.tile([P, N], U8, name="scale_rows", align_bytes=64)
        scale_dealt = keep.tile([P, N], U8, name="scale_dealt", align_bytes=64)
        zero_beside_gpsimd(rk_pool[0 : P - 1, 0:ZEROED_EARLY].bitcast(I32))
        nc.vector.tensor_copy(scale_rows[:], scale_pool[:].indirect(offsets[:]))
        zero_beside_gpsimd(rk_pool[0 : P - 1, ZEROED_EARLY:ZEROED].bitcast(I32))

        def place_scales():
            nc.vector.tensor_copy(
                scale_dealt[:, 0:HALF].bitcast(I32).rearrange("p (k j w) -> p k j w", k=4, w=2),
                scale_rows[:, 0:HALF].bitcast(I32).rearrange("p (j k w) -> p k j w", k=4, w=2),
            )
            nc.vector.tensor_copy(
                scale_dealt[:, HALF:N].bitcast(I32).rearrange("p (c k j w) -> p c k j w", c=2, k=2, w=4),
                scale_rows[:, HALF:N].bitcast(I32).rearrange("p (c j k w) -> p c k j w", c=2, k=2, w=4),
            )
            for o in range(PASSES):
                for j in range(4):
                    row = 16 * o + j
                    nc.sync.dma_start(
                        planes[o][j:P:32, :].bitcast(I32), scale_dealt[row : row + 13 : 4, :].bitcast(I32)
                    )

        place_scales()
        q_bf = {}
        q_codes = [keep.tile([P, NQ], U32, name=f"q_codes{o}", align_bytes=64) for o in range(PASSES)]
        q_scales = [keep.tile([P, NQ], U8, name=f"q_scales{o}", align_bytes=64) for o in range(PASSES)]

        def cast(o, tag):
            q_bf[o] = keep.tile([P, NQ, 4], BF16, name=f"q_bf{o}", tag=tag, align_bytes=64)
            nc.scalar.copy(
                q_bf[o][:].rearrange("p (c i) j -> p c j i", i=4), q_raw[o][:].rearrange("p j (c i) -> p c j i", i=4)
            )

        def quantize(o):
            nc.vector.quantize_mx(
                out=q_codes[o][:].bitcast(FP8X4), scales=q_scales[o][:], in_=q_bf[o][:].rearrange("p w j -> p (w j)")
            )

        cast(0, "early")
        turned = {}
        rk_dealt = keep.tile([P, N], F32, name="rk_dealt", tag="dealt")
        for h in range(2):
            rk_slots = keep.tile([P, HALF], F32, name=f"rk_slots{h}", tag=("words0", "late")[h], align_bytes=(32, 64)[h])
            nc.vector.tensor_copy(rk_slots[:], rk_pool[:].indirect(offsets[:, 32 * h : 32 * (h + 1)]))
            turned[h] = in_bank(6 + h, f"turned{h}")[:].rearrange("p (k m) -> p k m", m=P)
            groups = h + 1
            by_tile = rk_slots[:].rearrange("p (c j k s) -> p c k j s", c=groups, k=4 // groups, s=RUNS[h])
            for i in range(4):
                nc.scalar.activation(
                    rk_dealt[:, HALF * h + P * i : HALF * h + P * (i + 1)].rearrange("p (j s) -> p j s", s=RUNS[h]),
                    by_tile[:, i * groups // 4, i % (4 // groups)],
                    ACT.Copy,
                    scale=6.0,
                )
                nc.tensor.transpose(turned[h][:, i, :], rk_dealt[:, HALF * h + P * i : HALF * h + P * (i + 1)], ident[:])
        quantize(0)
        cast(1, "late")
        rk6 = shared.tile([P, TILES], F32, name="rk6", offset=0)
        for h in range(2):
            nc.scalar.copy(rk6[:, 4 * h : 4 * h + 4], turned[h][:, :, P - 1])

        first_keys = [
            keep.tile([P, 6, 2 * P], U8, name="first_keys0", align_bytes=64),
            shared.tile([P, 6, 2 * P], U8, name="first_keys1", offset=64, align_bytes=64),
        ]
        late_keys = keep.tile([P, 2, PASSES, 2 * P], U8, name="late_keys", align_bytes=64)
        words = [
            keep.tile([P, HALF], U32, name="words0", tag="words0", align_bytes=32),
            keep.tile([P, QUARTER], U32, name="words1"),
            shared.tile([P, QUARTER], U32, name="words2", offset=64 + 12 * P),
        ]
        starts = (0, HALF, HALF + QUARTER, N)

        def keys(k, o):
            return first_keys[o][:, k, :] if k < 6 else late_keys[:, k - 6, o, :]

        def gather_words(g):
            listed = offsets[:, starts[g] // 16 : starts[g + 1] // 16]
            nc.vector.tensor_copy(words[g][:], word_pool[:].bitcast(U32).indirect(listed))

        def halves(g):
            run = RUNS[min(g, 1)]
            return words[g][:].bitcast(U16).rearrange("p (j k s o) -> p k o j s", k=32 // run, s=run, o=PASSES)

        def split_pair(k, o):
            g = k // 4
            nc.vector.tensor_copy(
                first_keys[o][:, k : k + 2, :].bitcast(U16).rearrange("p k (j s) -> p k j s", s=RUNS[g]),
                halves(g)[:, k % 4 : k % 4 + 2, o],
            )

        def split(k):
            nc.vector.tensor_copy(
                late_keys[:, k - 6].bitcast(U16).rearrange("p o (j s) -> p o j s", s=RUNS[1]), halves(2)[:, k - 6]
            )

        match = [keep.tile([P, NQ], F32, name=f"match{k}") for k in range(TILES)]
        counts = keep.tile([P, N // SEG], F32, name="counts")

        def product(k, o, opens):
            nc.tensor.matmul_mx(
                out=scores[k],
                lhsT=keys(k, o).bitcast(FP4X4),
                lhsT_scale=planes[o][:, P * k : P * (k + 1)],
                rhs=q_codes[o][:].bitcast(FP8X4),
                rhs_scale=q_scales[o][:],
                start=opens,
                stop=not opens,
            )

        def weigh(k):
            nc.scalar.activation(match[k][:], scores[k], ACT.Sigmoid, bias=shift[:], scale=rk6[:, k : k + 1])

        def count(first, run, summed):
            nc.vector.tensor_reduce(
                counts[:, first : first + P // run],
                summed.rearrange("p (j s) -> p j s", s=run),
                mybir.AxisListType.X,
                mybir.AluOpType.add,
            )

        gather_words(0)
        gather_words(1)
        scores = [in_bank(k, f"scores{k}")[:, 0:NQ] for k in range(TILES)]
        for k in (0, 2, 4):
            split_pair(k, 0)
        quantize(1)
        for k in (0, 2):
            split_pair(k, 1)
        gather_words(2)
        split_pair(4, 1)
        for k in (6, 7):
            split(k)
        for k in range(6):
            product(k, 0, True)
        for k in range(6):
            product(k, 1, False)
            weigh(k)
        for k in (6, 7):
            product(k, 1, True)
            product(k, 0, False)
            weigh(k)

        pairs = []
        for k in (0, 2):
            pair = keep.tile([P, NQ], F32, name=f"pair{k}")
            nc.vector.tensor_add(pair[:], match[k][:], match[k + 1][:])
            pairs.append(pair)

        def turn_and_count(bank, terms, first, run):
            summed = in_bank(bank, f"summed{bank}")[:, 0:P]
            for i, term in enumerate(terms):
                nc.tensor.matmul(summed, term[:], ident[:], start=i == 0, stop=i == 1, is_transpose=True)
            count(first, run, summed)

        turn_and_count(4, pairs, 0, RUNS[0])
        turn_and_count(3, match[4:6], 16, RUNS[1])
        turn_and_count(2, match[6:8], 24, RUNS[1])
        nc.sync.dma_start(out[0], counts[:])
